import numpy as np
import ml_dtypes


def mxq(x, axis, fmt="e4m3"):
    dtype, down = {"e4m3": (ml_dtypes.float8_e4m3fn, 7), "e5m2": (ml_dtypes.float8_e5m2, 14)}[fmt]
    v = np.moveaxis(np.asarray(x, np.float32).astype(ml_dtypes.bfloat16).astype(np.float64), axis, -1)
    blocks = v.reshape(v.shape[:-1] + (-1, 32))
    amax = np.abs(blocks).max(-1, keepdims=True)
    byte = np.maximum(np.where(amax > 0, np.frexp(amax)[1] - 1 + 127, 0) - down, 1)
    scale = np.exp2(byte - 127.0)
    codes = (blocks / scale).astype(np.float32).astype(dtype).astype(np.float64)
    return np.moveaxis((codes * scale).reshape(v.shape), -1, axis)


WIDE = False


def mx_kscale(k):
    if not WIDE:
        return np.ones(k)
    levels = np.array([10, -10, 5, -5, 0])
    if k % 512:
        return np.exp2(np.random.permutation(np.resize(levels, k // 32))).repeat(32)
    a = np.empty((k // 512, 16))
    for p in range(k // 512):
        a[p, :8] = np.random.permutation(np.resize(levels, 8))
        for g in range(8):
            far = levels[np.abs(levels - a[p, g]) >= 10]
            a[p, g + 8] = far[np.random.randint(len(far))]
    return np.exp2(a.ravel()).repeat(32)


def f64(x):
    return np.asarray(x).astype(np.float64)


def striped(idx):
    return np.tile(idx.reshape(-1, 16).T, (8, 1)).astype(np.uint16)


def unstriped(offs):
    return offs[:16].T.reshape(-1).astype(np.int64)


E2M1 = np.array([0.0, 0.5, 1.0, 1.5, 2.0, 3.0, 4.0, 6.0, -0.0, -0.5, -1.0, -1.5, -2.0, -3.0, -4.0, -6.0])


def pack_weight(w, fmt):
    k, n = w.shape
    w = f64(np.asarray(w, np.float32).astype(ml_dtypes.bfloat16)).reshape(k // 32, 32, n)
    amax = np.abs(w).max(1)
    if fmt == "e4m3":
        byte = np.frexp(amax)[1] - 1 + 127 - 7
    else:
        mant, ex = np.frexp(amax / 6.0)
        byte = np.where(mant > 0.5, ex, ex - 1) + 127
    byte = np.clip(np.where(amax > 0, byte, 1), 1, 254)
    scaled = (w * np.exp2(127.0 - byte)[:, None, :]).reshape(k, n).astype(np.float32)
    by_word = np.ascontiguousarray(scaled.reshape(k // 512, 128, 4, n).transpose(0, 1, 3, 2))
    if fmt == "e4m3":
        words = by_word.astype(ml_dtypes.float8_e4m3fn).view(np.uint8)
    else:
        c = by_word.astype(ml_dtypes.float4_e2m1fn).view(np.uint8) & 0xF
        words = (c[..., 0::2] | (c[..., 1::2] << 4)).reshape(k // 512, 128, 2 * n)
    return np.ascontiguousarray(words), np.ascontiguousarray(byte.astype(np.uint8).reshape(k // 512, 16, n))


def unpack_weight(words, scales, fmt):
    g, _, n = scales.shape
    words = np.ascontiguousarray(words).reshape(g, 128, n, -1)
    if fmt == "e4m3":
        vals = words.view(ml_dtypes.float8_e4m3fn).astype(np.float64)
    else:
        nib = np.empty((g, 128, n, 4), np.uint8)
        nib[..., 0::2] = words & 0xF
        nib[..., 1::2] = words >> 4
        vals = E2M1[nib]
    vals = vals * np.repeat(np.exp2(scales.astype(np.float64) - 127.0), 8, axis=1)[..., None]
    return vals.transpose(0, 1, 3, 2).reshape(g * 512, n)


def gelu(v):
    return 0.5 * v * (1.0 + np.tanh(np.sqrt(2.0 / np.pi) * (v + 0.044715 * v**3)))


K, H, T, S, T2, P = 1024, 1024, 2048, 512, 1024, 512

def setup_inputs():
    n = np.random.standard_normal
    s = mx_kscale(K)[:, None]
    u = mx_kscale(H)[:, None]
    tab_words, tab_scales = pack_weight(n((K, T)) * s, "e4m3")
    w4_words, w4_scales = pack_weight(n((K, H)) / np.sqrt(K) / s * u.T, "e2m1")
    w8_words, w8_scales = pack_weight(n((K, H)) / np.sqrt(K) / s * u.T, "e4m3")
    return {
        "tab_words": tab_words, "tab_scales": tab_scales,
        "offs": striped(np.random.permutation(T)[:S]),
        "offs2": striped(np.random.permutation(T2)[:S]),
        "offs3": striped(np.random.permutation(T2)[:P]),
        "offs4": striped(np.random.permutation(T2)[:P]),
        "w1": (n((K, H)) / np.sqrt(K) / s * u.T).astype(np.float32),
        "w4_words": w4_words, "w4_scales": w4_scales,
        "w8_words": w8_words, "w8_scales": w8_scales,
        "page0": (n((H, T2)) * u).astype(np.float32),
        "wgs": np.exp(0.3 * n((128, S))).astype(np.float32),
        "gm": (n(H) / np.sqrt(H) / u[:, 0] ** 2).astype(np.float32),
        "bl": (0.7 * n(H) * u[:, 0]).astype(np.float32),
        "mix": (1.5 * n((P, P))).astype(np.float32),
    }

def reference(tab_words, tab_scales, offs, offs2, offs3, offs4, w1, w4_words, w4_scales, w8_words, w8_scales, page0, wgs, gm, bl, mix):
    v = unpack_weight(tab_words, tab_scales, "e4m3")[:, unstriped(offs)]
    w4 = unpack_weight(w4_words, w4_scales, "e2m1")
    w8 = unpack_weight(w8_words, w8_scales, "e4m3")
    ya = mxq(f64(w1), 0, "e4m3").T @ v
    yb = w4.T @ v
    yc = w8.T @ v
    h = np.maximum(np.maximum(ya, yb), yc)
    page = f64(page0).copy()
    page[:, unstriped(offs2)] = np.tile(f64(wgs), (H // 128, 1)) * h
    x1 = page[:, unstriped(offs3)] * f64(gm)[:, None]
    x2 = page[:, unstriped(offs4)] + f64(bl)[:, None]
    e = mxq(x1, 0, "e4m3").T @ mxq(x2, 0, "e4m3")
    return np.tanh(e) * f64(mix) + e

@@ -1,0 +1,335 @@
+from contextlib import ExitStack
+
+import concourse.mybir as mybir
+from concourse.masks import make_identity
+
+K, H, T, S, T2, NP = 1024, 1024, 2048, 512, 1024, 512
+FLOPS = 3 * 2 * K * H * S + 2 * H * NP * NP
+
+F32 = mybir.dt.float32
+BF16 = mybir.dt.bfloat16
+I32 = mybir.dt.int32
+U32 = mybir.dt.uint32
+U16 = mybir.dt.uint16
+U8 = mybir.dt.uint8
+FP8X4 = mybir.dt.float8_e4m3fn_x4
+FP4X4 = mybir.dt.float4_e2m1fn_x4
+ALU = mybir.AluOpType
+ACT = mybir.ActivationFunctionType
+
+P = 128
+W1_CHUNKS = ((0, 256), (256, 512), (512, 1024))
+WQ_CHUNKS = ((0, 256), (256, 1024))
+
+
+def chunk_of(chunks, col):
+    for k, (c0, c1) in enumerate(chunks):
+        if c0 <= col < c1:
+            return k, col - c0, c1 - c0
+    raise ValueError(col)
+
+
+def tile_list_peak_library_match_kernel(
+    tc, tab_words, tab_scales, offs, offs2, offs3, offs4, w1, w4_words, w4_scales,
+    w8_words, w8_scales, page0, wgs, gm, bl, mix, out,
+):
+    nc = tc.nc
+    with ExitStack() as ctx:
+        keep = ctx.enter_context(tc.tile_pool(name="keep", bufs=1))
+        ring = ctx.enter_context(tc.tile_pool(name="ring", bufs=2))
+        psum = ctx.enter_context(tc.psum_pool(name="psum", bufs=2))
+
+        lists = [keep.tile([P, 32], U16, name="list%d" % n) for n in range(4)]
+        tabw = [keep.tile([P, T], I32, name="tabw%d" % a, align_bytes=64) for a in range(2)]
+        tabs = keep.tile([P, 2 * T], U8, align_bytes=64)
+        w4s = keep.tile([P, 2 * H], U8, align_bytes=64)
+        w8s = keep.tile([P, 2 * H], U8, align_bytes=64)
+        w8s_rows = keep.tile([P, 2 * H], U8, align_bytes=64)
+        vecs = keep.tile([P, P], F32)
+        vec_rows = keep.tile([16, P], F32)
+        ident = keep.tile([P, P], F32)
+        ident_bf = keep.tile([P, P], BF16)
+        wg = keep.tile([P, S], F32)
+        page = [keep.tile([P, T2], F32, name="page%d" % n, align_bytes=64) for n in range(8)]
+        w1_raw = [[keep.tile([P, 4, c1 - c0], F32, name="w1raw%d%d" % (k, a)) for a in range(2)]
+                  for k, (c0, c1) in enumerate(W1_CHUNKS)]
+        w8w = [keep.tile([P, 2 * (c1 - c0)], I32, name="w8w%d" % k, align_bytes=64) for k, (c0, c1) in enumerate(WQ_CHUNKS)]
+        w4w = [keep.tile([P, c1 - c0], I32, name="w4w%d" % k, align_bytes=64) for k, (c0, c1) in enumerate(WQ_CHUNKS)]
+        mix_sb = keep.tile([P, 4, NP], F32)
+
+        nc.vector.memset(tabs[:].bitcast(I32), 0)
+        nc.vector.memset(w4s[:].bitcast(I32), 0)
+        nc.vector.memset(w8s[:].bitcast(I32), 0)
+        nc.vector.memset(vecs[:], 0.0)
+
+        def load_scales(queue, dst, row0, src):
+            for q in range(4):
+                queue.dma_start(
+                    out=dst[32 * q + row0 : 32 * q + row0 + 4, :].bitcast(I32).rearrange("r (a c) -> r a c", a=2),
+                    in_=src[:, 4 * q : 4 * q + 4, :].bitcast(I32).rearrange("a r c -> r a c"),
+                )
+
+        load_scales(nc.gpsimd, tabs, 0, tab_scales)
+        load_scales(nc.gpsimd, w4s, 0, w4_scales)
+        make_identity(nc, ident[:])
+        make_identity(nc, ident_bf[:])
+
+        def load_tabw(a):
+            nc.sync.dma_start(out=tabw[a][:], in_=tab_words[a].rearrange("p t i -> p (t i)").bitcast(I32))
+
+        def load_w1(k):
+            c0, c1 = W1_CHUNKS[k]
+            for a in range(2):
+                nc.sync.dma_start(
+                    out=w1_raw[k][a][:],
+                    in_=w1[512 * a : 512 * a + 512, c0:c1].rearrange("(p i) c -> p i c", i=4),
+                )
+
+        def load_wq(k):
+            c0, c1 = WQ_CHUNKS[k]
+            nc.sync.dma_start(
+                out=w4w[k][:].rearrange("p (a c) -> p a c", a=2),
+                in_=w4_words.bitcast(I32)[:, :, c0 // 2 : c1 // 2].rearrange("a p c -> p a c"),
+            )
+            nc.sync.dma_start(
+                out=w8w[k][:].rearrange("p (a c) -> p a c", a=2),
+                in_=w8_words.rearrange("a p c i -> a p (c i)").bitcast(I32)[:, :, c0:c1].rearrange("a p c -> p a c"),
+            )
+
+        def load_page(n):
+            nc.sync.dma_start(out=page[n][:], in_=page0[P * n : P * n + P, :])
+
+        nc.sync.dma_start(lists[0][:], offs)
+        load_scales(nc.sync, w8s_rows, 0, w8_scales)
+        load_tabw(0)
+        load_wq(0)
+        load_tabw(1)
+        load_w1(0)
+        nc.sync.dma_start(out=wg[:], in_=wgs)
+        load_page(0)
+        nc.sync.dma_start(lists[1][:], offs2)
+        for v, vec in enumerate((gm, bl)):
+            nc.sync.dma_start(out=vec_rows[8 * v : 8 * v + 8, :], in_=vec.rearrange("(n p) -> n p", p=P))
+        load_w1(1)
+        nc.sync.dma_start(lists[3][:], offs4)
+        nc.sync.dma_start(lists[2][:], offs3)
+        load_page(1)
+        load_wq(1)
+        load_page(2)
+        load_w1(2)
+        for n in range(3, 8):
+            load_page(n)
+        nc.sync.dma_start(out=mix_sb[:], in_=mix.rearrange("(m p) j -> p m j", p=P))
+
+        vw, vs = [], []
+        for a in range(2):
+            vw_a = keep.tile([P, S], U32, name="vw%d" % a, align_bytes=64)
+            vs_a = keep.tile([P, S], U8, name="vs%d" % a, align_bytes=64)
+            vw.append(vw_a)
+            vs.append(vs_a)
+        for q in range(4):
+            rows = slice(32 * q, 32 * q + 4)
+            nc.vector.tensor_copy(out=w8s[rows, :].bitcast(I32), in_=w8s_rows[rows, :].bitcast(I32))
+        nc.vector.tensor_copy(vw[0][:], tabw[0][:].bitcast(U32).indirect(lists[0][:]))
+        for a in range(2):
+            nc.vector.tensor_copy(vs[a][:], tabs[:, T * a : T * a + T].indirect(lists[0][:]))
+
+        w1c = [keep.tile([P, 256], U32, name="w1c%d" % n, align_bytes=64) for n in range(8)]
+        w1s = [keep.tile([P, 256], U8, name="w1s%d" % n, align_bytes=64) for n in range(8)]
+        w1g = {}
+
+        def round_w1(n):
+            k, off, width = chunk_of(W1_CHUNKS, P * n)
+            g = ring.tile([P, 1024], BF16, tag="m%d" % (n % 2), name="w1g", bufs=1, align_bytes=64)
+            for a in range(2):
+                nc.scalar.copy(
+                    out=g[:, 512 * a : 512 * a + 512].rearrange("p (c e i) -> p c i e", e=4, i=4),
+                    in_=w1_raw[k][a][:, :, off : off + P].rearrange("p i (c e) -> p c i e", e=4),
+                )
+            w1g[n] = g
+
+        def quantize_w1(n):
+            nc.vector.quantize_mx(out=w1c[n][:].bitcast(FP8X4), scales=w1s[n][:], in_=w1g[n][:])
+
+        banks = {}
+
+        def products(n):
+            k, off, width = chunk_of(WQ_CHUNKS, P * n)
+            yb = psum.tile([P, S], F32, tag="a", name="yb", bufs=1)
+            yc = psum.tile([P, S], F32, tag="b", name="yc")
+            ya = psum.tile([P, S], F32, tag="c", name="ya")
+            for a in range(2):
+                c0 = 2 * (width * a + off)
+                nc.tensor.matmul_mx(
+                    out=yb[:], lhsT=w4w[k][:].bitcast(U8)[:, c0 : c0 + 256].bitcast(FP4X4),
+                    lhsT_scale=w4s[:, H * a + P * n : H * a + P * n + P],
+                    rhs=vw[a][:].bitcast(FP8X4), rhs_scale=vs[a][:], start=(a == 0), stop=(a == 1),
+                )
+            for a in range(2):
+                c0 = width * a + off
+                nc.tensor.matmul_mx(
+                    out=yc[:], lhsT=w8w[k][:, c0 : c0 + P].bitcast(FP8X4),
+                    lhsT_scale=w8s[:, H * a + P * n : H * a + P * n + P],
+                    rhs=vw[a][:].bitcast(FP8X4), rhs_scale=vs[a][:], start=(a == 0), stop=(a == 1),
+                )
+            for a in range(2):
+                nc.tensor.matmul_mx(
+                    out=ya[:], lhsT=w1c[n][:, P * a : P * a + P].bitcast(FP8X4), lhsT_scale=w1s[n][:, P * a : P * a + P],
+                    rhs=vw[a][:].bitcast(FP8X4), rhs_scale=vs[a][:], start=(a == 0), stop=(a == 1),
+                )
+            banks[n] = (yb, yc, ya)
+
+        ysb = {}
+
+        def copy_out(n):
+            y = ring.tile([P, S], F32, tag="y", name="ysb", bufs=1)
+            nc.scalar.copy(out=y[:], in_=banks[n][0][:])
+            ysb[n] = y
+
+        mab, hs = {}, {}
+
+        def max_ab(n):
+            m = ring.tile([P, S], F32, tag="m%d" % (n % 2), name="mab", bufs=1, align_bytes=64)
+            nc.vector.tensor_tensor(m[:], banks[n][1][:], ysb[n][:], ALU.max)
+            mab[n] = m
+
+        def max_abc(n):
+            h = ring.tile([P, S], F32, tag="h", name="h", align_bytes=64)
+            nc.vector.tensor_tensor(h[:], banks[n][2][:], mab[n][:], ALU.max)
+            hs[n] = h
+
+        def scatter(n):
+            nc.vector.tensor_tensor(page[n][:].indirect(lists[1][:]), hs[n][:], wg[:], ALU.mult)
+
+        cols = keep.tile([P, 16], F32)
+
+        def turn_vectors():
+            nc.scalar.copy(out=vecs[0:16, :], in_=vec_rows[:])
+            vec_ps = psum.tile([P, P], F32, tag="t2", name="vec_ps")
+            nc.tensor.transpose(vec_ps[:], vecs[:], ident[:])
+            nc.scalar.copy(out=cols[:], in_=vec_ps[:, 0:16])
+
+        xt = [[keep.tile([P, 4, 2, P], F32, name="xt%d%d" % (b, v)) for v in range(2)] for b in range(2)]
+
+        def fetch(n, v, c0, c1, tag, both):
+            b, q = divmod(n, 4)
+            w = P * (c1 - c0)
+            got = both[:, NP * v + P * c0 : NP * v + P * c1]
+            nc.vector.tensor_copy(got, page[n][:].indirect(lists[2 + v][:, 8 * c0 : 8 * c1]))
+            xb = ring.tile([P, NP], BF16, tag="xb", name="xb", bufs=3)
+            if v == 0:
+                nc.scalar.activation(xb[:, 0:w], got, ACT.Copy, scale=cols[:, n : n + 1])
+            else:
+                nc.scalar.activation(xb[:, 0:w], got, ACT.Identity, bias=cols[:, 8 + n : 9 + n])
+            turned = psum.tile([P, 4, P], BF16, tag=tag, name="turned", bufs=1)
+            for c in range(c1 - c0):
+                nc.tensor.transpose(turned[:, c, :], xb[:, P * c : P * c + P], ident_bf[:])
+            nc.scalar.copy(
+                out=xt[b][v][:, c0:c1, :, 32 * q : 32 * q + 32],
+                in_=turned[:, 0 : c1 - c0, :].bitcast(F32).rearrange("m c (p u) -> m c u p", u=2),
+            )
+
+        def turn_back(b, v, c0, c1):
+            xg = keep.tile([P, (c1 - c0) * 2 * P], F32, name="xg%d%d%d" % (b, v, c0), align_bytes=64)
+            for c in range(c0, c1, 2):
+                cn = min(2, c1 - c)
+                back = psum.tile([P, 2, 2, P], F32, tag="t2", name="back")
+                for d in range(cn):
+                    for u in range(2):
+                        nc.tensor.transpose(back[:, d, u, :], xt[b][v][:, c + d, u, :], ident[:])
+                nc.scalar.copy(
+                    out=xg[:, 2 * P * (c - c0) : 2 * P * (c - c0 + cn)].rearrange("p (d m u) -> p d m u", d=cn, u=2),
+                    in_=back[:, 0:cn].rearrange("p d u m -> p d m u"),
+                )
+            return xg
+
+        xs = [[keep.tile([P, NP], U8, name="xs%d%d" % (b, v), align_bytes=64) for v in range(2)] for b in range(2)]
+        xc = [[None, None], [keep.tile([P, NP], U32, name="xc1%d" % v, align_bytes=64) for v in range(2)]]
+
+        def quantize_x(b, v, c0, c1, xg):
+            nc.vector.quantize_mx(
+                out=xc[b][v][:, P * c0 : P * c1].bitcast(FP8X4), scales=xs[b][v][:, P * c0 : P * c1], in_=xg[:].bitcast(BF16)
+            )
+
+        round_w1(0)
+        quantize_w1(0)
+        nc.vector.tensor_copy(vw[1][:], tabw[1][:].bitcast(U32).indirect(lists[0][:]))
+        products(0)
+        copy_out(0)
+        round_w1(1)
+        max_ab(0)
+        quantize_w1(1)
+        max_abc(0)
+        products(1)
+        copy_out(1)
+        turn_vectors()
+        round_w1(2)
+        xg0 = {}
+        for n in range(8):
+            scatter(n)
+            if n + 2 < 8:
+                quantize_w1(n + 2)
+                products(n + 2)
+            if n + 1 < 8:
+                max_ab(n + 1)
+            both = ring.tile([P, 2 * NP], F32, tag="y", name="both", bufs=1)
+            if n < 7:
+                fetch(n, 1, 0, 4, "t1", both)
+            if n + 1 < 8:
+                max_abc(n + 1)
+            if n < 7:
+                fetch(n, 0, 0, 4, "t1", both)
+            if n + 2 < 8:
+                copy_out(n + 2)
+            if n + 3 < 8:
+                round_w1(n + 3)
+            if n in (4, 5):
+                xg0[5 - n] = turn_back(0, 5 - n, 0, 4)
+
+        pieces = ((0, 1), (1, 2), (2, 4))
+        fetch(7, 1, 0, 2, "t1", both)
+        fetch(7, 1, 2, 4, "a", both)
+        xg_moving = turn_back(1, 1, 0, 4)
+        xg_fixed = []
+        for k, (c0, c1) in enumerate(pieces):
+            fetch(7, 0, c0, c1, ("t1", "a")[k % 2], both)
+            xg_fixed.append(turn_back(1, 0, c0, c1))
+        e = [psum.tile([P, NP], F32, tag="bbcc"[m], name="e%d" % m) for m in range(4)]
+
+        def score(b, m):
+            nc.tensor.matmul_mx(
+                out=e[m][:], lhsT=xc[b][0][:, P * m : P * m + P].bitcast(FP8X4), lhsT_scale=xs[b][0][:, P * m : P * m + P],
+                rhs=xc[b][1][:].bitcast(FP8X4), rhs_scale=xs[b][1][:], start=(b == 0), stop=(b == 1),
+            )
+
+        for v in range(2):
+            xc[0][v] = ring.tile([P, NP], U32, tag="h", name="xc0", align_bytes=64)
+            quantize_x(0, v, 0, 4, xg0[v])
+        for m in range(4):
+            score(0, m)
+        quantize_x(1, 1, 0, 4, xg_moving)
+        for k, (c0, c1) in enumerate(pieces):
+            quantize_x(1, 0, c0, c1, xg_fixed[k])
+        ths = []
+        for m in range(4):
+            score(1, m)
+            th = ring.tile([P, NP], F32, tag="th", name="th", bufs=4)
+            nc.scalar.activation(th[:], e[m][:], ACT.Tanh)
+            ths.append(th)
+        prods = []
+
+        def weigh(m):
+            pr = ring.tile([P, NP], F32, tag="pr", name="pr")
+            nc.vector.tensor_tensor(pr[:], ths[m][:], mix_sb[:, m, :], ALU.mult)
+            prods.append(pr)
+
+        def finish(m):
+            res = ring.tile([P, NP], F32, tag="res", name="res", bufs=4)
+            nc.vector.tensor_tensor(res[:], e[m][:], prods[m][:], ALU.add)
+            nc.sync.dma_start(out=out[P * m : P * m + P, :], in_=res[:])
+
+        weigh(0)
+        for m in range(4):
+            if m + 1 < 4:
+                weigh(m + 1)
+            finish(m)

@@ -19,7 +19,7 @@ ACT = mybir.ActivationFunctionType
 
 P = 128
 W1_CHUNKS = ((0, 256), (256, 512), (512, 1024))
-WQ_CHUNKS = ((0, 256), (256, 1024))
+WQ_CHUNKS = ((0, 256), (256, 512), (512, 1024))
 
 
 def chunk_of(chunks, col):
@@ -44,80 +44,107 @@ def tile_list_peak_library_match_kernel(
         tabs = keep.tile([P, 2 * T], U8, align_bytes=64)
         w4s = keep.tile([P, 2 * H], U8, align_bytes=64)
         w8s = keep.tile([P, 2 * H], U8, align_bytes=64)
-        w8s_rows = keep.tile([P, 2 * H], U8, align_bytes=64)
         vecs = keep.tile([P, P], F32)
         vec_rows = keep.tile([16, P], F32)
         ident = keep.tile([P, P], F32)
         ident_bf = keep.tile([P, P], BF16)
         wg = keep.tile([P, S], F32)
-        page = [keep.tile([P, T2], F32, name="page%d" % n, align_bytes=64) for n in range(8)]
-        w1_raw = [[keep.tile([P, 4, c1 - c0], F32, name="w1raw%d%d" % (k, a)) for a in range(2)]
+        page = [keep.tile([P, T2], F32, name="page%d" % n, tag="slot%d" % n, align_bytes=64) for n in range(8)]
+        w1_raw = [[keep.tile([P, 4, c1 - c0], F32, name="w1raw%d%d" % (k, a), tag="w1raw%d%d" % (k, a)) for a in range(2)]
                   for k, (c0, c1) in enumerate(W1_CHUNKS)]
         w8w = [keep.tile([P, 2 * (c1 - c0)], I32, name="w8w%d" % k, align_bytes=64) for k, (c0, c1) in enumerate(WQ_CHUNKS)]
         w4w = [keep.tile([P, c1 - c0], I32, name="w4w%d" % k, align_bytes=64) for k, (c0, c1) in enumerate(WQ_CHUNKS)]
+        wgd = keep.tile([P, 4, S], F32, name="wgd")
         mix_sb = keep.tile([P, 4, NP], F32)
 
         nc.vector.memset(tabs[:].bitcast(I32), 0)
         nc.vector.memset(w4s[:].bitcast(I32), 0)
         nc.vector.memset(w8s[:].bitcast(I32), 0)
         nc.vector.memset(vecs[:], 0.0)
+        warm = keep.tile([P, 1], F32)
+        nc.scalar.activation(warm[:], vecs[:, 0:1], ACT.Tanh)
 
-        def load_scales(queue, dst, row0, src):
-            for q in range(4):
-                queue.dma_start(
+        def load_scales(dst, row0, src, quadrants):
+            for q in quadrants:
+                nc.sync.dma_start(
                     out=dst[32 * q + row0 : 32 * q + row0 + 4, :].bitcast(I32).rearrange("r (a c) -> r a c", a=2),
                     in_=src[:, 4 * q : 4 * q + 4, :].bitcast(I32).rearrange("a r c -> r a c"),
                 )
 
-        load_scales(nc.gpsimd, tabs, 0, tab_scales)
-        load_scales(nc.gpsimd, w4s, 0, w4_scales)
         make_identity(nc, ident[:])
         make_identity(nc, ident_bf[:])
 
         def load_tabw(a):
             nc.sync.dma_start(out=tabw[a][:], in_=tab_words[a].rearrange("p t i -> p (t i)").bitcast(I32))
 
-        def load_w1(k):
+        def load_w1(k, a):
             c0, c1 = W1_CHUNKS[k]
-            for a in range(2):
-                nc.sync.dma_start(
-                    out=w1_raw[k][a][:],
-                    in_=w1[512 * a : 512 * a + 512, c0:c1].rearrange("(p i) c -> p i c", i=4),
-                )
+            nc.sync.dma_start(
+                out=w1_raw[k][a][:],
+                in_=w1[512 * a : 512 * a + 512, c0:c1].rearrange("(p i) c -> p i c", i=4),
+            )
 
-        def load_wq(k):
+        def load_w4(k):
             c0, c1 = WQ_CHUNKS[k]
             nc.sync.dma_start(
                 out=w4w[k][:].rearrange("p (a c) -> p a c", a=2),
                 in_=w4_words.bitcast(I32)[:, :, c0 // 2 : c1 // 2].rearrange("a p c -> p a c"),
             )
+
+        def load_w8(k):
+            c0, c1 = WQ_CHUNKS[k]
             nc.sync.dma_start(
                 out=w8w[k][:].rearrange("p (a c) -> p a c", a=2),
                 in_=w8_words.rearrange("a p c i -> a p (c i)").bitcast(I32)[:, :, c0:c1].rearrange("a p c -> p a c"),
             )
 
         def load_page(n):
-            nc.sync.dma_start(out=page[n][:], in_=page0[P * n : P * n + P, :])
+            if n < 4:
+                rows = page0[P * n : P * n + P, :]
+            else:
+                rows = page0[512:H, :].rearrange("(g t i) c -> t g i c", t=4, i=8)[n - 4]
+            nc.sync.dma_start(out=page[n][:], in_=rows)
 
         nc.sync.dma_start(lists[0][:], offs)
-        load_scales(nc.sync, w8s_rows, 0, w8_scales)
         load_tabw(0)
-        load_wq(0)
+        load_scales(tabs, 0, tab_scales, range(4))
+        load_scales(w4s, 0, w4_scales, range(2))
         load_tabw(1)
-        load_w1(0)
+        load_scales(w4s, 0, w4_scales, range(2, 4))
+        load_w4(0)
+        load_w8(0)
+        load_w1(0, 0)
+        load_w1(0, 1)
+        load_scales(w8s, 4, w8_scales, range(4))
         nc.sync.dma_start(out=wg[:], in_=wgs)
         load_page(0)
         nc.sync.dma_start(lists[1][:], offs2)
         for v, vec in enumerate((gm, bl)):
-            nc.sync.dma_start(out=vec_rows[8 * v : 8 * v + 8, :], in_=vec.rearrange("(n p) -> n p", p=P))
-        load_w1(1)
+            nc.sync.dma_start(out=vec_rows[8 * v : 8 * v + 4, :], in_=vec[0:512].rearrange("(n p) -> n p", p=P))
+            nc.sync.dma_start(
+                out=vec_rows[8 * v + 4 : 8 * v + 8, :].rearrange("t (g i) -> t g i", i=8),
+                in_=vec[512:H].rearrange("(g t i) -> t g i", t=4, i=8),
+            )
+        load_w1(1, 0)
+        load_w1(1, 1)
         nc.sync.dma_start(lists[3][:], offs4)
         nc.sync.dma_start(lists[2][:], offs3)
         load_page(1)
-        load_wq(1)
+        load_w4(1)
+        load_w8(1)
+        load_w1(2, 0)
+        load_w1(2, 1)
         load_page(2)
-        load_w1(2)
-        for n in range(3, 8):
+        load_w4(2)
+        load_w8(2)
+        load_page(3)
+        load_page(4)
+        for g in range(16):
+            nc.sync.dma_start(
+                out=wgd[8 * g : 8 * g + 8, :, :],
+                in_=wgs[32 * (g % 4) : 32 * (g % 4) + 32, :].rearrange("(t i) j -> i t j", i=8),
+            )
+        for n in range(5, 8):
             load_page(n)
         nc.sync.dma_start(out=mix_sb[:], in_=mix.rearrange("(m p) j -> p m j", p=P))
 
@@ -127,9 +154,6 @@ def tile_list_peak_library_match_kernel(
             vs_a = keep.tile([P, S], U8, name="vs%d" % a, align_bytes=64)
             vw.append(vw_a)
             vs.append(vs_a)
-        for q in range(4):
-            rows = slice(32 * q, 32 * q + 4)
-            nc.vector.tensor_copy(out=w8s[rows, :].bitcast(I32), in_=w8s_rows[rows, :].bitcast(I32))
         nc.vector.tensor_copy(vw[0][:], tabw[0][:].bitcast(U32).indirect(lists[0][:]))
         for a in range(2):
             nc.vector.tensor_copy(vs[a][:], tabs[:, T * a : T * a + T].indirect(lists[0][:]))
@@ -140,11 +164,14 @@ def tile_list_peak_library_match_kernel(
 
         def round_w1(n):
             k, off, width = chunk_of(W1_CHUNKS, P * n)
-            g = ring.tile([P, 1024], BF16, tag="m%d" % (n % 2), name="w1g", bufs=1, align_bytes=64)
+            g = keep.tile([P, 1024], BF16, tag=("m0", "m1", "m1", "m0")[n] if n < 4 else "slot%d" % (n - 4), name="w1g", align_bytes=64)
             for a in range(2):
+                if n < 4:
+                    src = w1_raw[k][a][:, :, off : off + P].rearrange("p i (g h e) -> p g h i e", h=2, e=4)
+                else:
+                    src = w1_raw[k][a][:].rearrange("p i (g t h e) -> p t g h i e", t=4, h=2, e=4)[:, n - 4]
                 nc.scalar.copy(
-                    out=g[:, 512 * a : 512 * a + 512].rearrange("p (c e i) -> p c i e", e=4, i=4),
-                    in_=w1_raw[k][a][:, :, off : off + P].rearrange("p i (c e) -> p c i e", e=4),
+                    out=g[:, 512 * a : 512 * a + 512].rearrange("p (g h e i) -> p g h i e", h=2, e=4, i=4), in_=src
                 )
             w1g[n] = g
 
@@ -152,54 +179,73 @@ def tile_list_peak_library_match_kernel(
             nc.vector.quantize_mx(out=w1c[n][:].bitcast(FP8X4), scales=w1s[n][:], in_=w1g[n][:])
 
         banks = {}
+        w8d = keep.tile([P, 1024], I32, align_bytes=64, name="w8d")
+        w4d = keep.tile([P, 512], I32, align_bytes=64, name="w4d")
+        s4d = keep.tile([P, 1024], U8, align_bytes=64, name="s4d")
+        s8d = keep.tile([P, 1024], U8, align_bytes=64, name="s8d")
 
-        def products(n):
-            k, off, width = chunk_of(WQ_CHUNKS, P * n)
-            yb = psum.tile([P, S], F32, tag="a", name="yb", bufs=1)
-            yc = psum.tile([P, S], F32, tag="b", name="yc")
-            ya = psum.tile([P, S], F32, tag="c", name="ya")
-            for a in range(2):
-                c0 = 2 * (width * a + off)
-                nc.tensor.matmul_mx(
-                    out=yb[:], lhsT=w4w[k][:].bitcast(U8)[:, c0 : c0 + 256].bitcast(FP4X4),
-                    lhsT_scale=w4s[:, H * a + P * n : H * a + P * n + P],
-                    rhs=vw[a][:].bitcast(FP8X4), rhs_scale=vs[a][:], start=(a == 0), stop=(a == 1),
+        def deal_weights():
+            for dst, src, run in ((w4d, w4w[2], 4), (w8d, w8w[2], 8)):
+                nc.vector.tensor_copy(
+                    out=dst[:].rearrange("p (t g e) -> p t g e", t=4, e=run),
+                    in_=src[:].rearrange("p (g t e) -> p t g e", t=4, e=run),
                 )
-            for a in range(2):
-                c0 = width * a + off
-                nc.tensor.matmul_mx(
-                    out=yc[:], lhsT=w8w[k][:, c0 : c0 + P].bitcast(FP8X4),
-                    lhsT_scale=w8s[:, H * a + P * n : H * a + P * n + P],
-                    rhs=vw[a][:].bitcast(FP8X4), rhs_scale=vs[a][:], start=(a == 0), stop=(a == 1),
+
+        def deal_scales():
+            for dst, src in ((s4d, w4s), (s8d, w8s)):
+                nc.vector.tensor_copy(
+                    out=dst[:].bitcast(I32).rearrange("p (t a g e) -> p t a g e", t=4, a=2, e=2),
+                    in_=src[:].bitcast(I32).rearrange("p (a b g t e) -> p b t a g e", a=2, b=2, t=4, e=2)[:, 1],
                 )
+
+        def weight_operands(which, n, a):
+            if which == "a":
+                return w1c[n][:, P * a : P * a + P].bitcast(FP8X4), w1s[n][:, P * a : P * a + P]
+            if n < 4:
+                k, off, width = chunk_of(WQ_CHUNKS, P * n)
+                cw = slice(width * a + off, width * a + off + P)
+                cs = slice(H * a + P * n, H * a + P * n + P)
+                w4_words_sb, w8_words_sb, s4, s8 = w4w[k], w8w[k], w4s, w8s
+            else:
+                cw = cs = slice(256 * (n - 4) + P * a, 256 * (n - 4) + P * a + P)
+                w4_words_sb, w8_words_sb, s4, s8 = w4d, w8d, s4d, s8d
+            if which == "b":
+                return w4_words_sb[:].bitcast(U8)[:, 2 * cw.start : 2 * cw.stop].bitcast(FP4X4), s4[:, cs]
+            return w8_words_sb[:, cw].bitcast(FP8X4), s8[4:P, cs]
+
+        def products(n, kinds):
+            for which in kinds:
+                tag = {"b": "a", "c": "b", "a": "c" if n else "d"}[which]
+                banks[n, which] = psum.tile([P, S], F32, tag=tag, name="y" + which, bufs=1)
             for a in range(2):
-                nc.tensor.matmul_mx(
-                    out=ya[:], lhsT=w1c[n][:, P * a : P * a + P].bitcast(FP8X4), lhsT_scale=w1s[n][:, P * a : P * a + P],
-                    rhs=vw[a][:].bitcast(FP8X4), rhs_scale=vs[a][:], start=(a == 0), stop=(a == 1),
-                )
-            banks[n] = (yb, yc, ya)
+                for which in kinds:
+                    words, scales = weight_operands(which, n, a)
+                    nc.tensor.matmul_mx(
+                        out=banks[n, which][:], lhsT=words, lhsT_scale=scales,
+                        rhs=vw[a][:].bitcast(FP8X4), rhs_scale=vs[a][:], start=(a == 0), stop=(a == 1),
+                    )
 
         ysb = {}
 
         def copy_out(n):
-            y = ring.tile([P, S], F32, tag="y", name="ysb", bufs=1)
-            nc.scalar.copy(out=y[:], in_=banks[n][0][:])
+            y = (keep.tile([P, S], F32, tag="w1raw01", name="ysb") if n == 0 else ring.tile([P, S], F32, tag="y%d" % (n % 2), name="ysb", bufs=1))
+            nc.scalar.copy(out=y[:], in_=banks[n, "b"][:])
             ysb[n] = y
 
         mab, hs = {}, {}
 
         def max_ab(n):
-            m = ring.tile([P, S], F32, tag="m%d" % (n % 2), name="mab", bufs=1, align_bytes=64)
-            nc.vector.tensor_tensor(m[:], banks[n][1][:], ysb[n][:], ALU.max)
+            m = keep.tile([P, S], F32, tag="s%d" % ((n + 1) % 2) if n else "m0", name="mab", align_bytes=64)
+            nc.vector.tensor_tensor(m[:], banks[n, "c"][:], ysb[n][:], ALU.max)
             mab[n] = m
 
         def max_abc(n):
-            h = ring.tile([P, S], F32, tag="h", name="h", align_bytes=64)
-            nc.vector.tensor_tensor(h[:], banks[n][2][:], mab[n][:], ALU.max)
+            h = keep.tile([P, S], F32, tag="s%d" % (n % 2), name="h", align_bytes=64)
+            nc.vector.tensor_tensor(h[:], banks[n, "a"][:], mab[n][:], ALU.max)
             hs[n] = h
 
         def scatter(n):
-            nc.vector.tensor_tensor(page[n][:].indirect(lists[1][:]), hs[n][:], wg[:], ALU.mult)
+            nc.vector.tensor_tensor(page[n][:].indirect(lists[1][:]), hs[n][:], wg[:] if n < 4 else wgd[:, n - 4, :], ALU.mult)
 
         cols = keep.tile([P, 16], F32)
 
@@ -209,19 +255,26 @@ def tile_list_peak_library_match_kernel(
             nc.tensor.transpose(vec_ps[:], vecs[:], ident[:])
             nc.scalar.copy(out=cols[:], in_=vec_ps[:, 0:16])
 
-        xt = [[keep.tile([P, 4, 2, P], F32, name="xt%d%d" % (b, v)) for v in range(2)] for b in range(2)]
+        xt = [[keep.tile([P, 4, 2, P], F32, name="xt%d%d" % (b, v)) for v in range(2)] for b in range(1)]
+        xw = [keep.tile([P, 4 * NP], BF16, name="xw%d" % v, align_bytes=64) for v in range(2)]
 
         def fetch(n, v, c0, c1, tag, both):
             b, q = divmod(n, 4)
             w = P * (c1 - c0)
             got = both[:, NP * v + P * c0 : NP * v + P * c1]
             nc.vector.tensor_copy(got, page[n][:].indirect(lists[2 + v][:, 8 * c0 : 8 * c1]))
-            xb = ring.tile([P, NP], BF16, tag="xb", name="xb", bufs=3)
-            if v == 0:
-                nc.scalar.activation(xb[:, 0:w], got, ACT.Copy, scale=cols[:, n : n + 1])
+            if b == 0:
+                xb = ring.tile([P, NP], BF16, tag="xb", name="xb", bufs=3)
+                dst = xb[:, 0:w]
             else:
-                nc.scalar.activation(xb[:, 0:w], got, ACT.Identity, bias=cols[:, 8 + n : 9 + n])
-            turned = psum.tile([P, 4, P], BF16, tag=tag, name="turned", bufs=1)
+                dst = xw[v][:].rearrange("p (c t) -> p c t", t=4)[:, P * c0 : P * c1, q]
+            if v == 0:
+                nc.scalar.activation(dst, got, ACT.Copy, scale=cols[:, n : n + 1])
+            else:
+                nc.scalar.activation(dst, got, ACT.Identity, bias=cols[:, 8 + n : 9 + n])
+            if b == 1:
+                return
+            turned = psum.tile([P, 4, P], BF16, tag=tag, name="turned", bufs={"t1": 2, "a": 1, "b": 1, "c": 1}[tag])
             for c in range(c1 - c0):
                 nc.tensor.transpose(turned[:, c, :], xb[:, P * c : P * c + P], ident_bf[:])
             nc.scalar.copy(
@@ -244,72 +297,79 @@ def tile_list_peak_library_match_kernel(
             return xg
 
         xs = [[keep.tile([P, NP], U8, name="xs%d%d" % (b, v), align_bytes=64) for v in range(2)] for b in range(2)]
-        xc = [[None, None], [keep.tile([P, NP], U32, name="xc1%d" % v, align_bytes=64) for v in range(2)]]
+        xc = [[keep.tile([P, NP], U32, name="xc%d%d" % (b, v), align_bytes=64) for v in range(2)] for b in range(2)]
 
         def quantize_x(b, v, c0, c1, xg):
             nc.vector.quantize_mx(
-                out=xc[b][v][:, P * c0 : P * c1].bitcast(FP8X4), scales=xs[b][v][:, P * c0 : P * c1], in_=xg[:].bitcast(BF16)
+                out=xc[b][v][:, P * c0 : P * c1].bitcast(FP8X4), scales=xs[b][v][:, P * c0 : P * c1], in_=xg
             )
 
         round_w1(0)
         quantize_w1(0)
         nc.vector.tensor_copy(vw[1][:], tabw[1][:].bitcast(U32).indirect(lists[0][:]))
-        products(0)
-        copy_out(0)
+        products(0, "bca")
         round_w1(1)
+        copy_out(0)
         max_ab(0)
         quantize_w1(1)
         max_abc(0)
-        products(1)
+        products(1, "bca")
         copy_out(1)
         turn_vectors()
         round_w1(2)
         xg0 = {}
         for n in range(8):
             scatter(n)
-            if n + 2 < 8:
-                quantize_w1(n + 2)
-                products(n + 2)
             if n + 1 < 8:
                 max_ab(n + 1)
-            both = ring.tile([P, 2 * NP], F32, tag="y", name="both", bufs=1)
+            if n + 2 < 8:
+                quantize_w1(n + 2)
+                products(n + 2, "b")
+            both = ring.tile([P, 2 * NP], F32, tag="y%d" % ((n + 1) % 2), name="both", bufs=1)
             if n < 7:
                 fetch(n, 1, 0, 4, "t1", both)
+            if n + 2 < 8:
+                products(n + 2, "c")
             if n + 1 < 8:
                 max_abc(n + 1)
+            if n + 2 < 8:
+                products(n + 2, "a")
+            if n + 3 < 8:
+                round_w1(n + 3)
             if n < 7:
                 fetch(n, 0, 0, 4, "t1", both)
             if n + 2 < 8:
                 copy_out(n + 2)
-            if n + 3 < 8:
-                round_w1(n + 3)
-            if n in (4, 5):
-                xg0[5 - n] = turn_back(0, 5 - n, 0, 4)
+            if n == 4:
+                xg0[1] = turn_back(0, 1, 0, 4)
+            if n == 5:
+                xg0[0] = turn_back(0, 0, 0, 4)
+            if n == 0:
+                deal_scales()
+            if n == 1:
+                deal_weights()
+            if n in (5, 6):
+                quantize_x(0, 6 - n, 0, 4, xg0[6 - n][:].bitcast(BF16))
 
         pieces = ((0, 1), (1, 2), (2, 4))
-        fetch(7, 1, 0, 2, "t1", both)
-        fetch(7, 1, 2, 4, "a", both)
-        xg_moving = turn_back(1, 1, 0, 4)
-        xg_fixed = []
-        for k, (c0, c1) in enumerate(pieces):
-            fetch(7, 0, c0, c1, ("t1", "a")[k % 2], both)
-            xg_fixed.append(turn_back(1, 0, c0, c1))
-        e = [psum.tile([P, NP], F32, tag="bbcc"[m], name="e%d" % m) for m in range(4)]
+        fetch(7, 1, 0, 2, None, both)
+        fetch(7, 1, 2, 4, None, both)
+        for c0, c1 in pieces:
+            fetch(7, 0, c0, c1, None, both)
+        e = [psum.tile([P, NP], F32, tag="abcd"[m], name="e%d" % m, bufs=1) for m in range(4)]
 
         def score(b, m):
             nc.tensor.matmul_mx(
                 out=e[m][:], lhsT=xc[b][0][:, P * m : P * m + P].bitcast(FP8X4), lhsT_scale=xs[b][0][:, P * m : P * m + P],
-                rhs=xc[b][1][:].bitcast(FP8X4), rhs_scale=xs[b][1][:], start=(b == 0), stop=(b == 1),
+                rhs=xc[b][1][:, 0:NP].bitcast(FP8X4), rhs_scale=xs[b][1][:], start=(b == 0), stop=(b == 1),
             )
 
-        for v in range(2):
-            xc[0][v] = ring.tile([P, NP], U32, tag="h", name="xc0", align_bytes=64)
-            quantize_x(0, v, 0, 4, xg0[v])
         for m in range(4):
             score(0, m)
-        quantize_x(1, 1, 0, 4, xg_moving)
-        for k, (c0, c1) in enumerate(pieces):
-            quantize_x(1, 0, c0, c1, xg_fixed[k])
+        for c0, c1 in ((0, 2), (2, 4)):
+            quantize_x(1, 1, c0, c1, xw[1][:, 4 * P * c0 : 4 * P * c1])
+        for c0, c1 in pieces:
+            quantize_x(1, 0, c0, c1, xw[0][:, 4 * P * c0 : 4 * P * c1])
         ths = []
         for m in range(4):
             score(1, m)

@@ -45,7 +45,6 @@ def tile_list_peak_library_match_kernel(
         w4s = keep.tile([P, 2 * H], U8, align_bytes=64)
         w8s = keep.tile([P, 2 * H], U8, align_bytes=64)
         vecs = keep.tile([P, P], F32)
-        vec_rows = keep.tile([16, P], F32)
         ident = keep.tile([P, P], F32)
         ident_bf = keep.tile([P, P], BF16)
         wg = keep.tile([P, S], F32)
@@ -61,12 +60,10 @@ def tile_list_peak_library_match_kernel(
         nc.vector.memset(w4s[:].bitcast(I32), 0)
         nc.vector.memset(w8s[:].bitcast(I32), 0)
         nc.vector.memset(vecs[:], 0.0)
-        warm = keep.tile([P, 1], F32)
-        nc.scalar.activation(warm[:], vecs[:, 0:1], ACT.Tanh)
 
-        def load_scales(dst, row0, src, quadrants):
+        def load_scales(queue, dst, row0, src, quadrants):
             for q in quadrants:
-                nc.sync.dma_start(
+                queue.dma_start(
                     out=dst[32 * q + row0 : 32 * q + row0 + 4, :].bitcast(I32).rearrange("r (a c) -> r a c", a=2),
                     in_=src[:, 4 * q : 4 * q + 4, :].bitcast(I32).rearrange("a r c -> r a c"),
                 )
@@ -98,6 +95,12 @@ def tile_list_peak_library_match_kernel(
                 in_=w8_words.rearrange("a p c i -> a p (c i)").bitcast(I32)[:, :, c0:c1].rearrange("a p c -> p a c"),
             )
 
+        def load_wgs_dealt(t):
+            for q in range(4):
+                nc.sync.dma_start(
+                    out=wgd[32 * q : 32 * q + 32, t, :], in_=wgs.rearrange("(g t i) j -> t g i j", t=4, i=8)[t]
+                )
+
         def load_page(n):
             if n < 4:
                 rows = page0[P * n : P * n + P, :]
@@ -107,45 +110,47 @@ def tile_list_peak_library_match_kernel(
 
         nc.sync.dma_start(lists[0][:], offs)
         load_tabw(0)
-        load_scales(tabs, 0, tab_scales, range(4))
-        load_scales(w4s, 0, w4_scales, range(2))
+        load_scales(nc.sync, tabs, 0, tab_scales, range(0, 4))
+        load_scales(nc.sync, w4s, 0, w4_scales, range(0, 2))
         load_tabw(1)
-        load_scales(w4s, 0, w4_scales, range(2, 4))
+        load_scales(nc.sync, w4s, 0, w4_scales, range(2, 4))
         load_w4(0)
         load_w8(0)
+        load_scales(nc.sync, w8s, 4, w8_scales, range(0, 1))
         load_w1(0, 0)
+        load_scales(nc.sync, w8s, 4, w8_scales, range(1, 3))
         load_w1(0, 1)
-        load_scales(w8s, 4, w8_scales, range(4))
+        load_scales(nc.sync, w8s, 4, w8_scales, range(3, 4))
         nc.sync.dma_start(out=wg[:], in_=wgs)
         load_page(0)
         nc.sync.dma_start(lists[1][:], offs2)
-        for v, vec in enumerate((gm, bl)):
-            nc.sync.dma_start(out=vec_rows[8 * v : 8 * v + 4, :], in_=vec[0:512].rearrange("(n p) -> n p", p=P))
-            nc.sync.dma_start(
-                out=vec_rows[8 * v + 4 : 8 * v + 8, :].rearrange("t (g i) -> t g i", i=8),
-                in_=vec[512:H].rearrange("(g t i) -> t g i", t=4, i=8),
-            )
-        load_w1(1, 0)
-        load_w1(1, 1)
         nc.sync.dma_start(lists[3][:], offs4)
         nc.sync.dma_start(lists[2][:], offs3)
+        for v, vec in enumerate((gm, bl)):
+            nc.gpsimd.dma_start(out=vecs[8 * v : 8 * v + 4, :], in_=vec[0:512].rearrange("(n p) -> n p", p=P))
+            nc.gpsimd.dma_start(
+                out=vecs[8 * v + 4 : 8 * v + 8, :].rearrange("t (g i) -> t g i", i=8),
+                in_=vec[512:H].rearrange("(g t i) -> t g i", t=4, i=8),
+            )
         load_page(1)
+        load_w1(1,0)
+        load_w1(1,1)
         load_w4(1)
         load_w8(1)
-        load_w1(2, 0)
-        load_w1(2, 1)
         load_page(2)
+        load_w1(2,0)
+        load_w1(2,1)
         load_w4(2)
         load_w8(2)
         load_page(3)
+        load_wgs_dealt(0)
         load_page(4)
-        for g in range(16):
-            nc.sync.dma_start(
-                out=wgd[8 * g : 8 * g + 8, :, :],
-                in_=wgs[32 * (g % 4) : 32 * (g % 4) + 32, :].rearrange("(t i) j -> i t j", i=8),
-            )
-        for n in range(5, 8):
-            load_page(n)
+        load_wgs_dealt(1)
+        load_page(5)
+        load_wgs_dealt(2)
+        load_page(6)
+        load_wgs_dealt(3)
+        load_page(7)
         nc.sync.dma_start(out=mix_sb[:], in_=mix.rearrange("(m p) j -> p m j", p=P))
 
         vw, vs = [], []
@@ -215,7 +220,7 @@ def tile_list_peak_library_match_kernel(
 
         def products(n, kinds):
             for which in kinds:
-                tag = {"b": "a", "c": "b", "a": "c" if n else "d"}[which]
+                tag = {"b": "a", "c": "b", "a": "c"}[which]
                 banks[n, which] = psum.tile([P, S], F32, tag=tag, name="y" + which, bufs=1)
             for a in range(2):
                 for which in kinds:
@@ -235,12 +240,12 @@ def tile_list_peak_library_match_kernel(
         mab, hs = {}, {}
 
         def max_ab(n):
-            m = keep.tile([P, S], F32, tag="s%d" % ((n + 1) % 2) if n else "m0", name="mab", align_bytes=64)
+            m = keep.tile([P, S], F32, tag="m0" if n < 2 else "slot%d" % (n - 2), name="mab", align_bytes=64)
             nc.vector.tensor_tensor(m[:], banks[n, "c"][:], ysb[n][:], ALU.max)
             mab[n] = m
 
         def max_abc(n):
-            h = keep.tile([P, S], F32, tag="s%d" % (n % 2), name="h", align_bytes=64)
+            h = ring.tile([P, S], F32, tag="h", name="h", bufs=1, align_bytes=64)
             nc.vector.tensor_tensor(h[:], banks[n, "a"][:], mab[n][:], ALU.max)
             hs[n] = h
 
@@ -250,8 +255,7 @@ def tile_list_peak_library_match_kernel(
         cols = keep.tile([P, 16], F32)
 
         def turn_vectors():
-            nc.scalar.copy(out=vecs[0:16, :], in_=vec_rows[:])
-            vec_ps = psum.tile([P, P], F32, tag="t2", name="vec_ps")
+            vec_ps = psum.tile([P, P], F32, tag="c", name="vec_ps", bufs=1)
             nc.tensor.transpose(vec_ps[:], vecs[:], ident[:])
             nc.scalar.copy(out=cols[:], in_=vec_ps[:, 0:16])
 
@@ -313,9 +317,9 @@ def tile_list_peak_library_match_kernel(
         max_ab(0)
         quantize_w1(1)
         max_abc(0)
+        turn_vectors()
         products(1, "bca")
         copy_out(1)
-        turn_vectors()
         round_w1(2)
         xg0 = {}
         for n in range(8):

@@ -18,15 +18,15 @@ ALU = mybir.AluOpType
 ACT = mybir.ActivationFunctionType
 
 P = 128
-W1_CHUNKS = ((0, 256), (256, 512), (512, 1024))
-WQ_CHUNKS = ((0, 256), (256, 512), (512, 1024))
-
-
-def chunk_of(chunks, col):
-    for k, (c0, c1) in enumerate(chunks):
-        if c0 <= col < c1:
-            return k, col - c0, c1 - c0
-    raise ValueError(col)
+PASS = 512
+TILES = H // P
+PLAIN = PASS // P
+LAST = TILES - 1
+CHUNKS = ((0, 256), (256, 512), (512, 1024))
+DEALT = 2
+X1, X2 = 0, 1
+X2_PIECES = ((0, 2), (2, 4))
+X1_PIECES = ((0, 1), (1, 2), (2, 4))
 
 
 def tile_list_peak_library_match_kernel(
@@ -39,358 +39,345 @@ def tile_list_peak_library_match_kernel(
         ring = ctx.enter_context(tc.tile_pool(name="ring", bufs=2))
         psum = ctx.enter_context(tc.psum_pool(name="psum", bufs=2))
 
-        lists = [keep.tile([P, 32], U16, name="list%d" % n) for n in range(4)]
-        tabw = [keep.tile([P, T], I32, name="tabw%d" % a, align_bytes=64) for a in range(2)]
-        tabs = keep.tile([P, 2 * T], U8, align_bytes=64)
-        w4s = keep.tile([P, 2 * H], U8, align_bytes=64)
-        w8s = keep.tile([P, 2 * H], U8, align_bytes=64)
-        vecs = keep.tile([P, P], F32)
+        lists = [keep.tile([P, S // 16], U16, name="list%d" % n) for n in range(4)]
+        tab_w = [keep.tile([P, T], I32, name="tab_w%d" % a, align_bytes=64) for a in range(2)]
+        tab_s = keep.tile([P, 2 * T], U8, align_bytes=64)
+        w4_s = keep.tile([P, 2 * H], U8, align_bytes=64)
+        w8_s = keep.tile([P, 2 * H], U8, align_bytes=64)
+        vec_rows = keep.tile([P, P], F32)
         ident = keep.tile([P, P], F32)
         ident_bf = keep.tile([P, P], BF16)
-        wg = keep.tile([P, S], F32)
-        page = [keep.tile([P, T2], F32, name="page%d" % n, tag="slot%d" % n, align_bytes=64) for n in range(8)]
-        w1_raw = [[keep.tile([P, 4, c1 - c0], F32, name="w1raw%d%d" % (k, a), tag="w1raw%d%d" % (k, a)) for a in range(2)]
-                  for k, (c0, c1) in enumerate(W1_CHUNKS)]
-        w8w = [keep.tile([P, 2 * (c1 - c0)], I32, name="w8w%d" % k, align_bytes=64) for k, (c0, c1) in enumerate(WQ_CHUNKS)]
-        w4w = [keep.tile([P, c1 - c0], I32, name="w4w%d" % k, align_bytes=64) for k, (c0, c1) in enumerate(WQ_CHUNKS)]
-        wgd = keep.tile([P, 4, S], F32, name="wgd")
+        wgs_plain = keep.tile([P, S], F32)
+        page = [keep.tile([P, T2], F32, name="page%d" % n, tag="slot%d" % n, align_bytes=64) for n in range(TILES)]
+        w1_raw = [
+            [keep.tile([P, 4, c1 - c0], F32, name="w1_raw%d%d" % (k, a), tag="w1_raw%d%d" % (k, a)) for a in range(2)]
+            for k, (c0, c1) in enumerate(CHUNKS)
+        ]
+        w8_w = [keep.tile([P, 2 * (c1 - c0)], I32, name="w8_w%d" % k, align_bytes=64) for k, (c0, c1) in enumerate(CHUNKS)]
+        w4_w = [keep.tile([P, c1 - c0], I32, name="w4_w%d" % k, align_bytes=64) for k, (c0, c1) in enumerate(CHUNKS)]
+        wgs_dealt = keep.tile([P, 4, S], F32)
         mix_sb = keep.tile([P, 4, NP], F32)
 
-        nc.vector.memset(tabs[:].bitcast(I32), 0)
-        nc.vector.memset(w4s[:].bitcast(I32), 0)
-        nc.vector.memset(w8s[:].bitcast(I32), 0)
-        nc.vector.memset(vecs[:], 0.0)
+        nc.vector.memset(tab_s[:].bitcast(I32), 0)
+        nc.vector.memset(w4_s[:].bitcast(I32), 0)
+        nc.vector.memset(w8_s[:].bitcast(I32), 0)
+        nc.vector.memset(vec_rows[:], 0.0)
+        make_identity(nc, ident[:])
+        make_identity(nc, ident_bf[:])
 
-        def load_scales(queue, dst, row0, src, quadrants):
+        def load_scales(dst, row0, src, quadrants):
             for q in quadrants:
-                queue.dma_start(
+                nc.sync.dma_start(
                     out=dst[32 * q + row0 : 32 * q + row0 + 4, :].bitcast(I32).rearrange("r (a c) -> r a c", a=2),
                     in_=src[:, 4 * q : 4 * q + 4, :].bitcast(I32).rearrange("a r c -> r a c"),
                 )
 
-        make_identity(nc, ident[:])
-        make_identity(nc, ident_bf[:])
-
-        def load_tabw(a):
-            nc.sync.dma_start(out=tabw[a][:], in_=tab_words[a].rearrange("p t i -> p (t i)").bitcast(I32))
+        def load_tab_words(a):
+            nc.sync.dma_start(out=tab_w[a][:], in_=tab_words[a].rearrange("p t i -> p (t i)").bitcast(I32))
 
         def load_w1(k, a):
-            c0, c1 = W1_CHUNKS[k]
+            c0, c1 = CHUNKS[k]
             nc.sync.dma_start(
                 out=w1_raw[k][a][:],
-                in_=w1[512 * a : 512 * a + 512, c0:c1].rearrange("(p i) c -> p i c", i=4),
+                in_=w1[PASS * a : PASS * a + PASS, c0:c1].rearrange("(p i) c -> p i c", i=4),
             )
 
-        def load_w4(k):
-            c0, c1 = WQ_CHUNKS[k]
+        def load_packed_weights(k):
+            c0, c1 = CHUNKS[k]
             nc.sync.dma_start(
-                out=w4w[k][:].rearrange("p (a c) -> p a c", a=2),
+                out=w4_w[k][:].rearrange("p (a c) -> p a c", a=2),
                 in_=w4_words.bitcast(I32)[:, :, c0 // 2 : c1 // 2].rearrange("a p c -> p a c"),
             )
-
-        def load_w8(k):
-            c0, c1 = WQ_CHUNKS[k]
             nc.sync.dma_start(
-                out=w8w[k][:].rearrange("p (a c) -> p a c", a=2),
+                out=w8_w[k][:].rearrange("p (a c) -> p a c", a=2),
                 in_=w8_words.rearrange("a p c i -> a p (c i)").bitcast(I32)[:, :, c0:c1].rearrange("a p c -> p a c"),
             )
 
         def load_wgs_dealt(t):
             for q in range(4):
                 nc.sync.dma_start(
-                    out=wgd[32 * q : 32 * q + 32, t, :], in_=wgs.rearrange("(g t i) j -> t g i j", t=4, i=8)[t]
+                    out=wgs_dealt[32 * q : 32 * q + 32, t, :], in_=wgs.rearrange("(g t i) j -> t g i j", t=4, i=8)[t]
                 )
 
         def load_page(n):
-            if n < 4:
+            if n < PLAIN:
                 rows = page0[P * n : P * n + P, :]
             else:
-                rows = page0[512:H, :].rearrange("(g t i) c -> t g i c", t=4, i=8)[n - 4]
+                rows = page0[PASS:H, :].rearrange("(g t i) c -> t g i c", t=4, i=8)[n - PLAIN]
             nc.sync.dma_start(out=page[n][:], in_=rows)
 
         nc.sync.dma_start(lists[0][:], offs)
-        load_tabw(0)
-        load_scales(nc.sync, tabs, 0, tab_scales, range(0, 4))
-        load_scales(nc.sync, w4s, 0, w4_scales, range(0, 2))
-        load_tabw(1)
-        load_scales(nc.sync, w4s, 0, w4_scales, range(2, 4))
-        load_w4(0)
-        load_w8(0)
-        load_scales(nc.sync, w8s, 4, w8_scales, range(0, 1))
+        load_tab_words(0)
+        load_scales(tab_s, 0, tab_scales, range(0, 4))
+        load_scales(w4_s, 0, w4_scales, range(0, 2))
+        load_tab_words(1)
+        load_scales(w4_s, 0, w4_scales, range(2, 4))
+        load_packed_weights(0)
+        load_scales(w8_s, 4, w8_scales, range(0, 1))
         load_w1(0, 0)
-        load_scales(nc.sync, w8s, 4, w8_scales, range(1, 3))
+        load_scales(w8_s, 4, w8_scales, range(1, 3))
         load_w1(0, 1)
-        load_scales(nc.sync, w8s, 4, w8_scales, range(3, 4))
-        nc.sync.dma_start(out=wg[:], in_=wgs)
+        load_scales(w8_s, 4, w8_scales, range(3, 4))
+        nc.sync.dma_start(out=wgs_plain[:], in_=wgs)
         load_page(0)
         nc.sync.dma_start(lists[1][:], offs2)
         nc.sync.dma_start(lists[3][:], offs4)
         nc.sync.dma_start(lists[2][:], offs3)
         for v, vec in enumerate((gm, bl)):
-            nc.gpsimd.dma_start(out=vecs[8 * v : 8 * v + 4, :], in_=vec[0:512].rearrange("(n p) -> n p", p=P))
+            row = TILES * v
+            nc.gpsimd.dma_start(out=vec_rows[row : row + PLAIN, :], in_=vec[0:PASS].rearrange("(n p) -> n p", p=P))
             nc.gpsimd.dma_start(
-                out=vecs[8 * v + 4 : 8 * v + 8, :].rearrange("t (g i) -> t g i", i=8),
-                in_=vec[512:H].rearrange("(g t i) -> t g i", t=4, i=8),
+                out=vec_rows[row + PLAIN : row + TILES, :].rearrange("t (g i) -> t g i", i=8),
+                in_=vec[PASS:H].rearrange("(g t i) -> t g i", t=4, i=8),
             )
-        load_page(1)
-        load_w1(1,0)
-        load_w1(1,1)
-        load_w4(1)
-        load_w8(1)
-        load_page(2)
-        load_w1(2,0)
-        load_w1(2,1)
-        load_w4(2)
-        load_w8(2)
-        load_page(3)
-        load_wgs_dealt(0)
-        load_page(4)
-        load_wgs_dealt(1)
-        load_page(5)
-        load_wgs_dealt(2)
-        load_page(6)
-        load_wgs_dealt(3)
-        load_page(7)
+        for k in (1, 2):
+            load_page(k)
+            load_w1(k, 0)
+            load_w1(k, 1)
+            load_packed_weights(k)
+        load_page(PLAIN - 1)
+        for n in range(PLAIN, TILES):
+            load_wgs_dealt(n - PLAIN)
+            load_page(n)
         nc.sync.dma_start(out=mix_sb[:], in_=mix.rearrange("(m p) j -> p m j", p=P))
 
-        vw, vs = [], []
+        v_w, v_s = [], []
         for a in range(2):
-            vw_a = keep.tile([P, S], U32, name="vw%d" % a, align_bytes=64)
-            vs_a = keep.tile([P, S], U8, name="vs%d" % a, align_bytes=64)
-            vw.append(vw_a)
-            vs.append(vs_a)
-        nc.vector.tensor_copy(vw[0][:], tabw[0][:].bitcast(U32).indirect(lists[0][:]))
-        for a in range(2):
-            nc.vector.tensor_copy(vs[a][:], tabs[:, T * a : T * a + T].indirect(lists[0][:]))
+            v_w.append(keep.tile([P, S], U32, name="v_w%d" % a, align_bytes=64))
+            v_s.append(keep.tile([P, S], U8, name="v_s%d" % a, align_bytes=64))
 
-        w1c = [keep.tile([P, 256], U32, name="w1c%d" % n, align_bytes=64) for n in range(8)]
-        w1s = [keep.tile([P, 256], U8, name="w1s%d" % n, align_bytes=64) for n in range(8)]
-        w1g = {}
+        def gather_words(a):
+            nc.vector.tensor_copy(v_w[a][:], tab_w[a][:].bitcast(U32).indirect(lists[0][:]))
+
+        gather_words(0)
+        for a in range(2):
+            nc.vector.tensor_copy(v_s[a][:], tab_s[:, T * a : T * a + T].indirect(lists[0][:]))
+
+        w1_codes = [keep.tile([P, 2 * P], U32, name="w1_codes%d" % n, align_bytes=64) for n in range(TILES)]
+        w1_s = [keep.tile([P, 2 * P], U8, name="w1_s%d" % n, align_bytes=64) for n in range(TILES)]
+        w1_bf = {}
 
         def round_w1(n):
-            k, off, width = chunk_of(W1_CHUNKS, P * n)
-            g = keep.tile([P, 1024], BF16, tag=("m0", "m1", "m1", "m0")[n] if n < 4 else "slot%d" % (n - 4), name="w1g", align_bytes=64)
+            tag = ("m0", "m1", "m1", "m0")[n] if n < PLAIN else "slot%d" % (n - PLAIN)
+            rounded = keep.tile([P, 2 * PASS], BF16, tag=tag, name="w1_bf", align_bytes=64)
             for a in range(2):
-                if n < 4:
-                    src = w1_raw[k][a][:, :, off : off + P].rearrange("p i (g h e) -> p g h i e", h=2, e=4)
+                if n < PLAIN:
+                    off = P * (n % 2)
+                    src = w1_raw[n // 2][a][:, :, off : off + P].rearrange("p i (g h e) -> p g h i e", h=2, e=4)
                 else:
-                    src = w1_raw[k][a][:].rearrange("p i (g t h e) -> p t g h i e", t=4, h=2, e=4)[:, n - 4]
+                    src = w1_raw[DEALT][a][:].rearrange("p i (g t h e) -> p t g h i e", t=4, h=2, e=4)[:, n - PLAIN]
                 nc.scalar.copy(
-                    out=g[:, 512 * a : 512 * a + 512].rearrange("p (g h e i) -> p g h i e", h=2, e=4, i=4), in_=src
+                    out=rounded[:, PASS * a : PASS * a + PASS].rearrange("p (g h e i) -> p g h i e", h=2, e=4, i=4),
+                    in_=src,
                 )
-            w1g[n] = g
+            w1_bf[n] = rounded
 
         def quantize_w1(n):
-            nc.vector.quantize_mx(out=w1c[n][:].bitcast(FP8X4), scales=w1s[n][:], in_=w1g[n][:])
+            nc.vector.quantize_mx(out=w1_codes[n][:].bitcast(FP8X4), scales=w1_s[n][:], in_=w1_bf[n][:])
 
-        banks = {}
-        w8d = keep.tile([P, 1024], I32, align_bytes=64, name="w8d")
-        w4d = keep.tile([P, 512], I32, align_bytes=64, name="w4d")
-        s4d = keep.tile([P, 1024], U8, align_bytes=64, name="s4d")
-        s8d = keep.tile([P, 1024], U8, align_bytes=64, name="s8d")
+        words_dealt = {}
+        w4_s_dealt = keep.tile([P, 2 * PASS], U8, align_bytes=64)
+        w8_s_dealt = keep.tile([P, 2 * PASS], U8, align_bytes=64)
 
-        def deal_weights():
-            for dst, src, run in ((w4d, w4w[2], 4), (w8d, w8w[2], 8)):
-                nc.vector.tensor_copy(
+        def deal_words():
+            for weight, src, run, tag in (("w8", w8_w[DEALT], 8, "m1"), ("w4", w4_w[DEALT], 4, "m0")):
+                dst = words_dealt[weight] = keep.tile([P, P * run], I32, tag=tag, name="words_dealt", align_bytes=64)
+                nc.gpsimd.tensor_copy(
                     out=dst[:].rearrange("p (t g e) -> p t g e", t=4, e=run),
                     in_=src[:].rearrange("p (g t e) -> p t g e", t=4, e=run),
                 )
 
         def deal_scales():
-            for dst, src in ((s4d, w4s), (s8d, w8s)):
+            for dst, src in ((w4_s_dealt, w4_s), (w8_s_dealt, w8_s)):
                 nc.vector.tensor_copy(
                     out=dst[:].bitcast(I32).rearrange("p (t a g e) -> p t a g e", t=4, a=2, e=2),
                     in_=src[:].bitcast(I32).rearrange("p (a b g t e) -> p b t a g e", a=2, b=2, t=4, e=2)[:, 1],
                 )
 
-        def weight_operands(which, n, a):
-            if which == "a":
-                return w1c[n][:, P * a : P * a + P].bitcast(FP8X4), w1s[n][:, P * a : P * a + P]
-            if n < 4:
-                k, off, width = chunk_of(WQ_CHUNKS, P * n)
-                cw = slice(width * a + off, width * a + off + P)
-                cs = slice(H * a + P * n, H * a + P * n + P)
-                w4_words_sb, w8_words_sb, s4, s8 = w4w[k], w8w[k], w4s, w8s
+        def weight_operands(weight, n, a):
+            if weight == "w1":
+                return w1_codes[n][:, P * a : P * a + P].bitcast(FP8X4), w1_s[n][:, P * a : P * a + P]
+            if n < PLAIN:
+                first = 2 * P * a + P * (n % 2)
+                word_cols = slice(first, first + P)
+                scale_cols = slice(H * a + P * n, H * a + P * n + P)
+                words4, words8, scales4, scales8 = w4_w[n // 2], w8_w[n // 2], w4_s, w8_s
             else:
-                cw = cs = slice(256 * (n - 4) + P * a, 256 * (n - 4) + P * a + P)
-                w4_words_sb, w8_words_sb, s4, s8 = w4d, w8d, s4d, s8d
-            if which == "b":
-                return w4_words_sb[:].bitcast(U8)[:, 2 * cw.start : 2 * cw.stop].bitcast(FP4X4), s4[:, cs]
-            return w8_words_sb[:, cw].bitcast(FP8X4), s8[4:P, cs]
+                first = 2 * P * (n - PLAIN) + P * a
+                word_cols = scale_cols = slice(first, first + P)
+                words4, words8, scales4, scales8 = words_dealt["w4"], words_dealt["w8"], w4_s_dealt, w8_s_dealt
+            if weight == "w4":
+                return words4[:].bitcast(U8)[:, 2 * first : 2 * first + 2 * P].bitcast(FP4X4), scales4[:, scale_cols]
+            return words8[:, word_cols].bitcast(FP8X4), scales8[4:P, scale_cols]
 
-        def products(n, kinds):
-            for which in kinds:
-                tag = {"b": "a", "c": "b", "a": "c"}[which]
-                banks[n, which] = psum.tile([P, S], F32, tag=tag, name="y" + which, bufs=1)
+        product, w4_product_sb, two_max, h = {}, {}, {}, {}
+
+        def multiply(n, weights):
+            for weight in weights:
+                product[n, weight] = psum.tile([P, S], F32, tag=weight, name="product", bufs=1)
             for a in range(2):
-                for which in kinds:
-                    words, scales = weight_operands(which, n, a)
+                for weight in weights:
+                    words, scales = weight_operands(weight, n, a)
                     nc.tensor.matmul_mx(
-                        out=banks[n, which][:], lhsT=words, lhsT_scale=scales,
-                        rhs=vw[a][:].bitcast(FP8X4), rhs_scale=vs[a][:], start=(a == 0), stop=(a == 1),
+                        out=product[n, weight][:], lhsT=words, lhsT_scale=scales,
+                        rhs=v_w[a][:].bitcast(FP8X4), rhs_scale=v_s[a][:], start=(a == 0), stop=(a == 1),
                     )
 
-        ysb = {}
+        def copy_w4_product(n):
+            if n == 0:
+                w4_product_sb[n] = keep.tile([P, S], F32, tag="w1_raw01", name="w4_product_sb")
+            else:
+                w4_product_sb[n] = ring.tile([P, S], F32, tag="y%d" % (n % 2), name="w4_product_sb", bufs=1)
+            nc.scalar.copy(out=w4_product_sb[n][:], in_=product[n, "w4"][:])
 
-        def copy_out(n):
-            y = (keep.tile([P, S], F32, tag="w1raw01", name="ysb") if n == 0 else ring.tile([P, S], F32, tag="y%d" % (n % 2), name="ysb", bufs=1))
-            nc.scalar.copy(out=y[:], in_=banks[n, "b"][:])
-            ysb[n] = y
+        def max_of_two(n):
+            tag = "m0" if n < 2 else "slot%d" % (n - 2)
+            two_max[n] = keep.tile([P, S], F32, tag=tag, name="two_max", align_bytes=64)
+            nc.vector.tensor_tensor(two_max[n][:], product[n, "w8"][:], w4_product_sb[n][:], ALU.max)
 
-        mab, hs = {}, {}
-
-        def max_ab(n):
-            m = keep.tile([P, S], F32, tag="m0" if n < 2 else "slot%d" % (n - 2), name="mab", align_bytes=64)
-            nc.vector.tensor_tensor(m[:], banks[n, "c"][:], ysb[n][:], ALU.max)
-            mab[n] = m
-
-        def max_abc(n):
-            h = ring.tile([P, S], F32, tag="h", name="h", bufs=1, align_bytes=64)
-            nc.vector.tensor_tensor(h[:], banks[n, "a"][:], mab[n][:], ALU.max)
-            hs[n] = h
+        def max_of_three(n):
+            h[n] = ring.tile([P, S], F32, tag="h", name="h", bufs=1, align_bytes=64)
+            nc.vector.tensor_tensor(h[n][:], product[n, "w1"][:], two_max[n][:], ALU.max)
 
         def scatter(n):
-            nc.vector.tensor_tensor(page[n][:].indirect(lists[1][:]), hs[n][:], wg[:] if n < 4 else wgd[:, n - 4, :], ALU.mult)
+            factor = wgs_plain[:] if n < PLAIN else wgs_dealt[:, n - PLAIN, :]
+            nc.vector.tensor_tensor(page[n][:].indirect(lists[1][:]), h[n][:], factor, ALU.mult)
 
-        cols = keep.tile([P, 16], F32)
+        vec_cols = keep.tile([P, 2 * TILES], F32)
 
         def turn_vectors():
-            vec_ps = psum.tile([P, P], F32, tag="c", name="vec_ps", bufs=1)
-            nc.tensor.transpose(vec_ps[:], vecs[:], ident[:])
-            nc.scalar.copy(out=cols[:], in_=vec_ps[:, 0:16])
+            turned_vecs = psum.tile([P, P], F32, tag="w1", name="turned_vecs", bufs=1)
+            nc.tensor.transpose(turned_vecs[:], vec_rows[:], ident[:])
+            nc.scalar.copy(out=vec_cols[:], in_=turned_vecs[:, 0 : 2 * TILES])
 
-        xt = [[keep.tile([P, 4, 2, P], F32, name="xt%d%d" % (b, v)) for v in range(2)] for b in range(1)]
-        xw = [keep.tile([P, 4 * NP], BF16, name="xw%d" % v, align_bytes=64) for v in range(2)]
+        x_pairs = [keep.tile([P, 4, 2, P], F32, name="x_pairs%d" % v) for v in range(2)]
+        x_dealt = [keep.tile([P, 4 * NP], BF16, name="x_dealt%d" % v, align_bytes=64) for v in range(2)]
 
-        def fetch(n, v, c0, c1, tag, both):
-            b, q = divmod(n, 4)
-            w = P * (c1 - c0)
-            got = both[:, NP * v + P * c0 : NP * v + P * c1]
+        def fetch(n, v, c0, c1, fetched):
+            got = fetched[:, NP * v + P * c0 : NP * v + P * c1]
             nc.vector.tensor_copy(got, page[n][:].indirect(lists[2 + v][:, 8 * c0 : 8 * c1]))
-            if b == 0:
-                xb = ring.tile([P, NP], BF16, tag="xb", name="xb", bufs=3)
-                dst = xb[:, 0:w]
+            if n < PLAIN:
+                x_bf = ring.tile([P, NP], BF16, tag="x_bf", name="x_bf", bufs=3)
+                dst = x_bf[:]
             else:
-                dst = xw[v][:].rearrange("p (c t) -> p c t", t=4)[:, P * c0 : P * c1, q]
-            if v == 0:
-                nc.scalar.activation(dst, got, ACT.Copy, scale=cols[:, n : n + 1])
+                dst = x_dealt[v][:].rearrange("p (c t) -> p c t", t=4)[:, P * c0 : P * c1, n - PLAIN]
+            if v == X1:
+                nc.scalar.activation(dst, got, ACT.Copy, scale=vec_cols[:, n : n + 1])
             else:
-                nc.scalar.activation(dst, got, ACT.Identity, bias=cols[:, 8 + n : 9 + n])
-            if b == 1:
-                return
-            turned = psum.tile([P, 4, P], BF16, tag=tag, name="turned", bufs={"t1": 2, "a": 1, "b": 1, "c": 1}[tag])
-            for c in range(c1 - c0):
-                nc.tensor.transpose(turned[:, c, :], xb[:, P * c : P * c + P], ident_bf[:])
-            nc.scalar.copy(
-                out=xt[b][v][:, c0:c1, :, 32 * q : 32 * q + 32],
-                in_=turned[:, 0 : c1 - c0, :].bitcast(F32).rearrange("m c (p u) -> m c u p", u=2),
-            )
-
-        def turn_back(b, v, c0, c1):
-            xg = keep.tile([P, (c1 - c0) * 2 * P], F32, name="xg%d%d%d" % (b, v, c0), align_bytes=64)
-            for c in range(c0, c1, 2):
-                cn = min(2, c1 - c)
-                back = psum.tile([P, 2, 2, P], F32, tag="t2", name="back")
-                for d in range(cn):
-                    for u in range(2):
-                        nc.tensor.transpose(back[:, d, u, :], xt[b][v][:, c + d, u, :], ident[:])
+                nc.scalar.activation(dst, got, ACT.Identity, bias=vec_cols[:, TILES + n : TILES + n + 1])
+            if n < PLAIN:
+                turned = psum.tile([P, 4, P], BF16, tag="turned", name="turned")
+                for c in range(4):
+                    nc.tensor.transpose(turned[:, c, :], x_bf[:, P * c : P * c + P], ident_bf[:])
                 nc.scalar.copy(
-                    out=xg[:, 2 * P * (c - c0) : 2 * P * (c - c0 + cn)].rearrange("p (d m u) -> p d m u", d=cn, u=2),
-                    in_=back[:, 0:cn].rearrange("p d u m -> p d m u"),
+                    out=x_pairs[v][:, :, :, 32 * n : 32 * n + 32],
+                    in_=turned[:].bitcast(F32).rearrange("m c (p u) -> m c u p", u=2),
                 )
-            return xg
 
-        xs = [[keep.tile([P, NP], U8, name="xs%d%d" % (b, v), align_bytes=64) for v in range(2)] for b in range(2)]
-        xc = [[keep.tile([P, NP], U32, name="xc%d%d" % (b, v), align_bytes=64) for v in range(2)] for b in range(2)]
+        def turn_back(v):
+            pairs = keep.tile([P, 2 * NP], F32, name="x_turned_back%d" % v, align_bytes=64)
+            for c in (0, 2):
+                back = psum.tile([P, 2, 2, P], F32, tag="back", name="back")
+                for d in range(2):
+                    for u in range(2):
+                        nc.tensor.transpose(back[:, d, u, :], x_pairs[v][:, c + d, u, :], ident[:])
+                nc.scalar.copy(
+                    out=pairs[:, 2 * P * c : 2 * P * (c + 2)].rearrange("p (d m u) -> p d m u", d=2, u=2),
+                    in_=back[:].rearrange("p d u m -> p d m u"),
+                )
+            return pairs
 
-        def quantize_x(b, v, c0, c1, xg):
-            nc.vector.quantize_mx(
-                out=xc[b][v][:, P * c0 : P * c1].bitcast(FP8X4), scales=xs[b][v][:, P * c0 : P * c1], in_=xg
-            )
+        x_s = [[keep.tile([P, NP], U8, name="x_s%d%d" % (b, v), align_bytes=64) for v in range(2)] for b in range(2)]
+        x_codes = [[keep.tile([P, NP], U32, name="x_codes%d%d" % (b, v), align_bytes=64) for v in range(2)] for b in range(2)]
+
+        def quantize_x(b, v, c0, c1, values):
+            cols = slice(P * c0, P * c1)
+            nc.vector.quantize_mx(out=x_codes[b][v][:, cols].bitcast(FP8X4), scales=x_s[b][v][:, cols], in_=values)
 
         round_w1(0)
         quantize_w1(0)
-        nc.vector.tensor_copy(vw[1][:], tabw[1][:].bitcast(U32).indirect(lists[0][:]))
-        products(0, "bca")
+        gather_words(1)
+        multiply(0, ("w4", "w8", "w1"))
         round_w1(1)
-        copy_out(0)
-        max_ab(0)
+        copy_w4_product(0)
+        max_of_two(0)
         quantize_w1(1)
-        max_abc(0)
+        max_of_three(0)
         turn_vectors()
-        products(1, "bca")
-        copy_out(1)
+        multiply(1, ("w4", "w8", "w1"))
+        copy_w4_product(1)
         round_w1(2)
-        xg0 = {}
-        for n in range(8):
+
+        turned_back = {}
+        for n in range(TILES):
             scatter(n)
-            if n + 1 < 8:
-                max_ab(n + 1)
-            if n + 2 < 8:
+            if n + 1 < TILES:
+                max_of_two(n + 1)
+            if n + 2 < TILES:
                 quantize_w1(n + 2)
-                products(n + 2, "b")
-            both = ring.tile([P, 2 * NP], F32, tag="y%d" % ((n + 1) % 2), name="both", bufs=1)
-            if n < 7:
-                fetch(n, 1, 0, 4, "t1", both)
-            if n + 2 < 8:
-                products(n + 2, "c")
-            if n + 1 < 8:
-                max_abc(n + 1)
-            if n + 2 < 8:
-                products(n + 2, "a")
-            if n + 3 < 8:
+                multiply(n + 2, ("w4",))
+            fetched = ring.tile([P, 2 * NP], F32, tag="y%d" % ((n + 1) % 2), name="fetched", bufs=1)
+            if n < LAST:
+                fetch(n, X2, 0, 4, fetched)
+            if n + 2 < TILES:
+                multiply(n + 2, ("w8",))
+            if n + 1 < TILES:
+                max_of_three(n + 1)
+            if n + 2 < TILES:
+                multiply(n + 2, ("w1",))
+            if n + 3 < TILES:
                 round_w1(n + 3)
-            if n < 7:
-                fetch(n, 0, 0, 4, "t1", both)
-            if n + 2 < 8:
-                copy_out(n + 2)
-            if n == 4:
-                xg0[1] = turn_back(0, 1, 0, 4)
-            if n == 5:
-                xg0[0] = turn_back(0, 0, 0, 4)
+            if n < LAST:
+                fetch(n, X1, 0, 4, fetched)
+            if n + 2 < TILES:
+                copy_w4_product(n + 2)
+            if n == PLAIN:
+                turned_back[X2] = turn_back(X2)
+            if n == PLAIN + 1:
+                turned_back[X1] = turn_back(X1)
             if n == 0:
                 deal_scales()
             if n == 1:
-                deal_weights()
-            if n in (5, 6):
-                quantize_x(0, 6 - n, 0, 4, xg0[6 - n][:].bitcast(BF16))
+                deal_words()
+            if n == PLAIN + 1:
+                quantize_x(0, X2, 0, 4, turned_back[X2][:].bitcast(BF16))
+            if n == PLAIN + 2:
+                quantize_x(0, X1, 0, 4, turned_back[X1][:].bitcast(BF16))
 
-        pieces = ((0, 1), (1, 2), (2, 4))
-        fetch(7, 1, 0, 2, None, both)
-        fetch(7, 1, 2, 4, None, both)
-        for c0, c1 in pieces:
-            fetch(7, 0, c0, c1, None, both)
-        e = [psum.tile([P, NP], F32, tag="abcd"[m], name="e%d" % m, bufs=1) for m in range(4)]
+        for c0, c1 in X2_PIECES:
+            fetch(LAST, X2, c0, c1, fetched)
+        for c0, c1 in X1_PIECES:
+            fetch(LAST, X1, c0, c1, fetched)
+
+        e = [psum.tile([P, NP], F32, tag=tag, name="e%d" % m, bufs=1) for m, tag in enumerate(("w4", "w8", "w1", "e3"))]
 
         def score(b, m):
+            peaks = slice(P * m, P * m + P)
             nc.tensor.matmul_mx(
-                out=e[m][:], lhsT=xc[b][0][:, P * m : P * m + P].bitcast(FP8X4), lhsT_scale=xs[b][0][:, P * m : P * m + P],
-                rhs=xc[b][1][:, 0:NP].bitcast(FP8X4), rhs_scale=xs[b][1][:], start=(b == 0), stop=(b == 1),
+                out=e[m][:], lhsT=x_codes[b][X1][:, peaks].bitcast(FP8X4), lhsT_scale=x_s[b][X1][:, peaks],
+                rhs=x_codes[b][X2][:].bitcast(FP8X4), rhs_scale=x_s[b][X2][:], start=(b == 0), stop=(b == 1),
             )
 
         for m in range(4):
             score(0, m)
-        for c0, c1 in ((0, 2), (2, 4)):
-            quantize_x(1, 1, c0, c1, xw[1][:, 4 * P * c0 : 4 * P * c1])
-        for c0, c1 in pieces:
-            quantize_x(1, 0, c0, c1, xw[0][:, 4 * P * c0 : 4 * P * c1])
-        ths = []
+        for v, pieces in ((X2, X2_PIECES), (X1, X1_PIECES)):
+            for c0, c1 in pieces:
+                quantize_x(1, v, c0, c1, x_dealt[v][:, 4 * P * c0 : 4 * P * c1])
+        tanh_e = []
         for m in range(4):
             score(1, m)
-            th = ring.tile([P, NP], F32, tag="th", name="th", bufs=4)
-            nc.scalar.activation(th[:], e[m][:], ACT.Tanh)
-            ths.append(th)
-        prods = []
+            tanh_e.append(ring.tile([P, NP], F32, tag="tanh_e", name="tanh_e", bufs=4))
+            nc.scalar.activation(tanh_e[m][:], e[m][:], ACT.Tanh)
+        weighed = []
 
         def weigh(m):
-            pr = ring.tile([P, NP], F32, tag="pr", name="pr")
-            nc.vector.tensor_tensor(pr[:], ths[m][:], mix_sb[:, m, :], ALU.mult)
-            prods.append(pr)
+            weighed.append(ring.tile([P, NP], F32, tag="weighed", name="weighed"))
+            nc.vector.tensor_tensor(weighed[m][:], tanh_e[m][:], mix_sb[:, m, :], ALU.mult)
 
         def finish(m):
-            res = ring.tile([P, NP], F32, tag="res", name="res", bufs=4)
-            nc.vector.tensor_tensor(res[:], e[m][:], prods[m][:], ALU.add)
-            nc.sync.dma_start(out=out[P * m : P * m + P, :], in_=res[:])
+            result = ring.tile([P, NP], F32, tag="result", name="result", bufs=4)
+            nc.vector.tensor_tensor(result[:], e[m][:], weighed[m][:], ALU.add)
+            nc.sync.dma_start(out=out[P * m : P * m + P, :], in_=result[:])
 
         weigh(0)
         for m in range(4):

@@ -24,9 +24,11 @@ PLAIN = PASS // P
 LAST = TILES - 1
 CHUNKS = ((0, 256), (256, 512), (512, 1024))
 DEALT = 2
+WEIGHTS = ("w4", "w8", "w1")
 X1, X2 = 0, 1
-X2_PIECES = ((0, 2), (2, 4))
-X1_PIECES = ((0, 1), (1, 2), (2, 4))
+LAST_PIECES = tuple((v, c, c + 2) for c in (0, 2) for v in (X2, X1))
+PART = NP // 2
+OUT_PARTS = tuple((m, j0) for m0 in (0, 2) for j0 in (0, PART) for m in (m0, m0 + 1))
 
 
 def tile_list_peak_library_match_kernel(
@@ -53,8 +55,9 @@ def tile_list_peak_library_match_kernel(
             [keep.tile([P, 4, c1 - c0], F32, name="w1_raw%d%d" % (k, a), tag="w1_raw%d%d" % (k, a)) for a in range(2)]
             for k, (c0, c1) in enumerate(CHUNKS)
         ]
-        w8_w = [keep.tile([P, 2 * (c1 - c0)], I32, name="w8_w%d" % k, align_bytes=64) for k, (c0, c1) in enumerate(CHUNKS)]
-        w4_w = [keep.tile([P, c1 - c0], I32, name="w4_w%d" % k, align_bytes=64) for k, (c0, c1) in enumerate(CHUNKS)]
+        widths = [c1 - c0 for c0, c1 in CHUNKS]
+        w8_w = [keep.tile([P, 2 * w], I32, name="w8_w", tag="w8_w%d" % k, align_bytes=64) for k, w in enumerate(widths)]
+        w4_w = [keep.tile([P, w], I32, name="w4_w", tag="w4_w%d" % k, align_bytes=64) for k, w in enumerate(widths)]
         wgs_dealt = keep.tile([P, 4, S], F32)
         mix_sb = keep.tile([P, 4, NP], F32)
 
@@ -123,8 +126,7 @@ def tile_list_peak_library_match_kernel(
         nc.sync.dma_start(lists[1][:], offs2)
         nc.sync.dma_start(lists[3][:], offs4)
         nc.sync.dma_start(lists[2][:], offs3)
-        for v, vec in enumerate((gm, bl)):
-            row = TILES * v
+        for row, vec in ((0, gm), (TILES, bl)):
             nc.gpsimd.dma_start(out=vec_rows[row : row + PLAIN, :], in_=vec[0:PASS].rearrange("(n p) -> n p", p=P))
             nc.gpsimd.dma_start(
                 out=vec_rows[row + PLAIN : row + TILES, :].rearrange("t (g i) -> t g i", i=8),
@@ -146,10 +148,11 @@ def tile_list_peak_library_match_kernel(
             v_w.append(keep.tile([P, S], U32, name="v_w%d" % a, align_bytes=64))
             v_s.append(keep.tile([P, S], U8, name="v_s%d" % a, align_bytes=64))
 
-        def gather_words(a):
-            nc.vector.tensor_copy(v_w[a][:], tab_w[a][:].bitcast(U32).indirect(lists[0][:]))
+        def gather_words(a, j0, j1):
+            entries = lists[0][:, j0 // 16 : j1 // 16]
+            nc.vector.tensor_copy(v_w[a][:, j0:j1], tab_w[a][:].bitcast(U32).indirect(entries))
 
-        gather_words(0)
+        gather_words(0, 0, S)
         for a in range(2):
             nc.vector.tensor_copy(v_s[a][:], tab_s[:, T * a : T * a + T].indirect(lists[0][:]))
 
@@ -158,7 +161,7 @@ def tile_list_peak_library_match_kernel(
         w1_bf = {}
 
         def round_w1(n):
-            tag = ("m0", "m1", "m1", "m0")[n] if n < PLAIN else "slot%d" % (n - PLAIN)
+            tag = ("spare0", "spare1", "spare1", "spare0")[n] if n < PLAIN else "slot%d" % (n - PLAIN)
             rounded = keep.tile([P, 2 * PASS], BF16, tag=tag, name="w1_bf", align_bytes=64)
             for a in range(2):
                 if n < PLAIN:
@@ -176,11 +179,10 @@ def tile_list_peak_library_match_kernel(
             nc.vector.quantize_mx(out=w1_codes[n][:].bitcast(FP8X4), scales=w1_s[n][:], in_=w1_bf[n][:])
 
         words_dealt = {}
-        w4_s_dealt = keep.tile([P, 2 * PASS], U8, align_bytes=64)
-        w8_s_dealt = keep.tile([P, 2 * PASS], U8, align_bytes=64)
+        scales_dealt = {}
 
         def deal_words():
-            for weight, src, run, tag in (("w8", w8_w[DEALT], 8, "m1"), ("w4", w4_w[DEALT], 4, "m0")):
+            for weight, src, run, tag in (("w8", w8_w[DEALT], 8, "spare1"), ("w4", w4_w[DEALT], 4, "spare0")):
                 dst = words_dealt[weight] = keep.tile([P, P * run], I32, tag=tag, name="words_dealt", align_bytes=64)
                 nc.gpsimd.tensor_copy(
                     out=dst[:].rearrange("p (t g e) -> p t g e", t=4, e=run),
@@ -188,8 +190,10 @@ def tile_list_peak_library_match_kernel(
                 )
 
         def deal_scales():
-            for dst, src in ((w4_s_dealt, w4_s), (w8_s_dealt, w8_s)):
-                nc.vector.tensor_copy(
+            for weight, src in (("w4", w4_s), ("w8", w8_s)):
+                tag = "%s_w%d" % (weight, DEALT)
+                dst = scales_dealt[weight] = keep.tile([P, 2 * PASS], U8, tag=tag, name="scales_dealt", align_bytes=64)
+                nc.gpsimd.tensor_copy(
                     out=dst[:].bitcast(I32).rearrange("p (t a g e) -> p t a g e", t=4, a=2, e=2),
                     in_=src[:].bitcast(I32).rearrange("p (a b g t e) -> p b t a g e", a=2, b=2, t=4, e=2)[:, 1],
                 )
@@ -198,16 +202,17 @@ def tile_list_peak_library_match_kernel(
             if weight == "w1":
                 return w1_codes[n][:, P * a : P * a + P].bitcast(FP8X4), w1_s[n][:, P * a : P * a + P]
             if n < PLAIN:
-                first = 2 * P * a + P * (n % 2)
-                word_cols = slice(first, first + P)
+                col0 = 2 * P * a + P * (n % 2)
+                word_cols = slice(col0, col0 + P)
                 scale_cols = slice(H * a + P * n, H * a + P * n + P)
                 words4, words8, scales4, scales8 = w4_w[n // 2], w8_w[n // 2], w4_s, w8_s
             else:
-                first = 2 * P * (n - PLAIN) + P * a
-                word_cols = scale_cols = slice(first, first + P)
-                words4, words8, scales4, scales8 = words_dealt["w4"], words_dealt["w8"], w4_s_dealt, w8_s_dealt
+                col0 = 2 * P * (n - PLAIN) + P * a
+                word_cols = scale_cols = slice(col0, col0 + P)
+                words4, words8 = words_dealt["w4"], words_dealt["w8"]
+                scales4, scales8 = scales_dealt["w4"], scales_dealt["w8"]
             if weight == "w4":
-                return words4[:].bitcast(U8)[:, 2 * first : 2 * first + 2 * P].bitcast(FP4X4), scales4[:, scale_cols]
+                return words4[:].bitcast(U8)[:, 2 * col0 : 2 * col0 + 2 * P].bitcast(FP4X4), scales4[:, scale_cols]
             return words8[:, word_cols].bitcast(FP8X4), scales8[4:P, scale_cols]
 
         product, w4_product_sb, two_max, h = {}, {}, {}, {}
@@ -224,14 +229,11 @@ def tile_list_peak_library_match_kernel(
                     )
 
         def copy_w4_product(n):
-            if n == 0:
-                w4_product_sb[n] = keep.tile([P, S], F32, tag="w1_raw01", name="w4_product_sb")
-            else:
-                w4_product_sb[n] = ring.tile([P, S], F32, tag="y%d" % (n % 2), name="w4_product_sb", bufs=1)
+            w4_product_sb[n] = ring.tile([P, S], F32, tag="turn%d" % (n % 2), name="w4_product_sb", bufs=1)
             nc.scalar.copy(out=w4_product_sb[n][:], in_=product[n, "w4"][:])
 
         def max_of_two(n):
-            tag = "m0" if n < 2 else "slot%d" % (n - 2)
+            tag = "spare0" if n == 1 else "slot%d" % (n - 2)
             two_max[n] = keep.tile([P, S], F32, tag=tag, name="two_max", align_bytes=64)
             nc.vector.tensor_tensor(two_max[n][:], product[n, "w8"][:], w4_product_sb[n][:], ALU.max)
 
@@ -288,7 +290,9 @@ def tile_list_peak_library_match_kernel(
             return pairs
 
         x_s = [[keep.tile([P, NP], U8, name="x_s%d%d" % (b, v), align_bytes=64) for v in range(2)] for b in range(2)]
-        x_codes = [[keep.tile([P, NP], U32, name="x_codes%d%d" % (b, v), align_bytes=64) for v in range(2)] for b in range(2)]
+        x_codes = [
+            [keep.tile([P, NP], U32, name="x_codes%d%d" % (b, v), align_bytes=64) for v in range(2)] for b in range(2)
+        ]
 
         def quantize_x(b, v, c0, c1, values):
             cols = slice(P * c0, P * c1)
@@ -296,27 +300,48 @@ def tile_list_peak_library_match_kernel(
 
         round_w1(0)
         quantize_w1(0)
-        gather_words(1)
-        multiply(0, ("w4", "w8", "w1"))
+        halves = (slice(0, S // 2), slice(S // 2, S))
+        first = {}
+        for half, tags in zip(halves, ((("w4", 1), ("w8", 1), ("w1", 1)), (("back", 2), ("back", 2), ("extra", 1)))):
+            gather_words(1, half.start, half.stop)
+            for weight, (tag, bufs) in zip(WEIGHTS, tags):
+                first[half.start, weight] = psum.tile([P, S // 2], F32, tag=tag, name="first", bufs=bufs)
+            for a in range(2):
+                for weight in WEIGHTS:
+                    words, scales = weight_operands(weight, 0, a)
+                    nc.tensor.matmul_mx(
+                        out=first[half.start, weight][:], lhsT=words, lhsT_scale=scales,
+                        rhs=v_w[a][:, half].bitcast(FP8X4), rhs_scale=v_s[a][:, half], start=(a == 0), stop=(a == 1),
+                    )
         round_w1(1)
-        copy_w4_product(0)
-        max_of_two(0)
+        first_sb = keep.tile([P, S], F32, tag="w1_raw01", name="first_sb")
+        first_two = keep.tile([P, S], F32, tag="spare0", name="first_two", align_bytes=64)
+        h[0] = ring.tile([P, S], F32, tag="h", name="h", bufs=1, align_bytes=64)
+        for half in halves:
+            nc.scalar.copy(out=first_sb[:, half], in_=first[half.start, "w4"][:])
+        for half in halves:
+            nc.vector.tensor_tensor(first_two[:, half], first[half.start, "w8"][:], first_sb[:, half], ALU.max)
+        for half in halves:
+            nc.vector.tensor_tensor(h[0][:, half], first[half.start, "w1"][:], first_two[:, half], ALU.max)
+        for half in halves:
+            places = lists[1][:, half.start // 16 : half.stop // 16]
+            nc.vector.tensor_tensor(page[0][:].indirect(places), h[0][:, half], wgs_plain[:, half], ALU.mult)
         quantize_w1(1)
-        max_of_three(0)
         turn_vectors()
-        multiply(1, ("w4", "w8", "w1"))
+        multiply(1, WEIGHTS)
         copy_w4_product(1)
         round_w1(2)
 
         turned_back = {}
         for n in range(TILES):
-            scatter(n)
+            if n > 0:
+                scatter(n)
             if n + 1 < TILES:
                 max_of_two(n + 1)
             if n + 2 < TILES:
                 quantize_w1(n + 2)
                 multiply(n + 2, ("w4",))
-            fetched = ring.tile([P, 2 * NP], F32, tag="y%d" % ((n + 1) % 2), name="fetched", bufs=1)
+            fetched = ring.tile([P, 2 * NP], F32, tag="turn%d" % ((n + 1) % 2), name="fetched", bufs=1)
             if n < LAST:
                 fetch(n, X2, 0, 4, fetched)
             if n + 2 < TILES:
@@ -335,52 +360,54 @@ def tile_list_peak_library_match_kernel(
                 turned_back[X2] = turn_back(X2)
             if n == PLAIN + 1:
                 turned_back[X1] = turn_back(X1)
-            if n == 0:
-                deal_scales()
-            if n == 1:
+            if n == PLAIN - 3:
                 deal_words()
+                deal_scales()
             if n == PLAIN + 1:
                 quantize_x(0, X2, 0, 4, turned_back[X2][:].bitcast(BF16))
             if n == PLAIN + 2:
                 quantize_x(0, X1, 0, 4, turned_back[X1][:].bitcast(BF16))
 
-        for c0, c1 in X2_PIECES:
-            fetch(LAST, X2, c0, c1, fetched)
-        for c0, c1 in X1_PIECES:
-            fetch(LAST, X1, c0, c1, fetched)
+        for v, c0, c1 in LAST_PIECES:
+            fetch(LAST, v, c0, c1, fetched)
 
-        e = [psum.tile([P, NP], F32, tag=tag, name="e%d" % m, bufs=1) for m, tag in enumerate(("w4", "w8", "w1", "e3"))]
+        banks = (("w4", 1), ("w8", 1), ("w1", 1), ("extra", 1), ("back", 2), ("back", 2), ("turned", 2), ("turned", 2))
+        e = [psum.tile([P, PART], F32, tag=tag, name="e", bufs=bufs) for tag, bufs in banks]
+        parts = range(len(OUT_PARTS))
 
-        def score(b, m):
-            peaks = slice(P * m, P * m + P)
+        def score(b, part):
+            m, j0 = OUT_PARTS[part]
+            peaks, compounds = slice(P * m, P * m + P), slice(j0, j0 + PART)
             nc.tensor.matmul_mx(
-                out=e[m][:], lhsT=x_codes[b][X1][:, peaks].bitcast(FP8X4), lhsT_scale=x_s[b][X1][:, peaks],
-                rhs=x_codes[b][X2][:].bitcast(FP8X4), rhs_scale=x_s[b][X2][:], start=(b == 0), stop=(b == 1),
+                out=e[part][:], lhsT=x_codes[b][X1][:, peaks].bitcast(FP8X4), lhsT_scale=x_s[b][X1][:, peaks],
+                rhs=x_codes[b][X2][:, compounds].bitcast(FP8X4), rhs_scale=x_s[b][X2][:, compounds],
+                start=(b == 0), stop=(b == 1),
             )
 
-        for m in range(4):
-            score(0, m)
-        for v, pieces in ((X2, X2_PIECES), (X1, X1_PIECES)):
-            for c0, c1 in pieces:
-                quantize_x(1, v, c0, c1, x_dealt[v][:, 4 * P * c0 : 4 * P * c1])
+        for part in parts:
+            score(0, part)
+        for v, c0, c1 in LAST_PIECES:
+            quantize_x(1, v, c0, c1, x_dealt[v][:, 4 * P * c0 : 4 * P * c1])
         tanh_e = []
-        for m in range(4):
-            score(1, m)
-            tanh_e.append(ring.tile([P, NP], F32, tag="tanh_e", name="tanh_e", bufs=4))
-            nc.scalar.activation(tanh_e[m][:], e[m][:], ACT.Tanh)
+        for part in parts:
+            score(1, part)
+            tanh_e.append(keep.tile([P, PART], F32, name="tanh_e%d" % part))
+            nc.scalar.activation(tanh_e[part][:], e[part][:], ACT.Tanh)
         weighed = []
 
-        def weigh(m):
-            weighed.append(ring.tile([P, NP], F32, tag="weighed", name="weighed"))
-            nc.vector.tensor_tensor(weighed[m][:], tanh_e[m][:], mix_sb[:, m, :], ALU.mult)
+        def weigh(part):
+            m, j0 = OUT_PARTS[part]
+            weighed.append(ring.tile([P, PART], F32, tag="weighed", name="weighed"))
+            nc.vector.tensor_tensor(weighed[part][:], tanh_e[part][:], mix_sb[:, m, j0 : j0 + PART], ALU.mult)
 
-        def finish(m):
-            result = ring.tile([P, NP], F32, tag="result", name="result", bufs=4)
-            nc.vector.tensor_tensor(result[:], e[m][:], weighed[m][:], ALU.add)
-            nc.sync.dma_start(out=out[P * m : P * m + P, :], in_=result[:])
+        def finish(part):
+            m, j0 = OUT_PARTS[part]
+            result = keep.tile([P, PART], F32, name="result%d" % part)
+            nc.vector.tensor_tensor(result[:], e[part][:], weighed[part][:], ALU.add)
+            nc.sync.dma_start(out=out[P * m : P * m + P, j0 : j0 + PART], in_=result[:])
 
         weigh(0)
-        for m in range(4):
-            if m + 1 < 4:
-                weigh(m + 1)
-            finish(m)
+        for part in parts:
+            if part + 1 < len(parts):
+                weigh(part + 1)
+            finish(part)

from contextlib import ExitStack

import concourse.mybir as mybir
from concourse.masks import make_identity

K, H, T, S, T2, NP = 1024, 1024, 2048, 512, 1024, 512
FLOPS = 3 * 2 * K * H * S + 2 * H * NP * NP

F32 = mybir.dt.float32
BF16 = mybir.dt.bfloat16
I32 = mybir.dt.int32
U32 = mybir.dt.uint32
U16 = mybir.dt.uint16
U8 = mybir.dt.uint8
FP8X4 = mybir.dt.float8_e4m3fn_x4
FP4X4 = mybir.dt.float4_e2m1fn_x4
ALU = mybir.AluOpType
ACT = mybir.ActivationFunctionType

P = 128
PASS = 512
TILES = H // P
PLAIN = PASS // P
LAST = TILES - 1
CHUNKS = ((0, 256), (256, 512), (512, 1024))
DEALT = 2
WEIGHTS = ("w4", "w8", "w1")
X1, X2 = 0, 1
LAST_PIECES = tuple((v, c, c + 2) for c in (0, 2) for v in (X2, X1))
PART = NP // 2
OUT_PARTS = tuple((m, j0) for m0 in (0, 2) for j0 in (0, PART) for m in (m0, m0 + 1))


def tile_list_peak_library_match_kernel(
    tc, tab_words, tab_scales, offs, offs2, offs3, offs4, w1, w4_words, w4_scales,
    w8_words, w8_scales, page0, wgs, gm, bl, mix, out,
):
    nc = tc.nc
    with ExitStack() as ctx:
        keep = ctx.enter_context(tc.tile_pool(name="keep", bufs=1))
        ring = ctx.enter_context(tc.tile_pool(name="ring", bufs=2))
        psum = ctx.enter_context(tc.psum_pool(name="psum", bufs=2))

        lists = [keep.tile([P, S // 16], U16, name="list%d" % n) for n in range(4)]
        tab_w = [keep.tile([P, T], I32, name="tab_w%d" % a, align_bytes=64) for a in range(2)]
        tab_s = keep.tile([P, 2 * T], U8, align_bytes=64)
        w4_s = keep.tile([P, 2 * H], U8, align_bytes=64)
        w8_s = keep.tile([P, 2 * H], U8, align_bytes=64)
        vec_rows = keep.tile([P, P], F32)
        ident = keep.tile([P, P], F32)
        ident_bf = keep.tile([P, P], BF16)
        wgs_plain = keep.tile([P, S], F32)
        page = [keep.tile([P, T2], F32, name="page%d" % n, tag="slot%d" % n, align_bytes=64) for n in range(TILES)]
        w1_raw = [
            [keep.tile([P, 4, c1 - c0], F32, name="w1_raw%d%d" % (k, a), tag="w1_raw%d%d" % (k, a)) for a in range(2)]
            for k, (c0, c1) in enumerate(CHUNKS)
        ]
        widths = [c1 - c0 for c0, c1 in CHUNKS]
        w8_w = [keep.tile([P, 2 * w], I32, name="w8_w", tag="w8_w%d" % k, align_bytes=64) for k, w in enumerate(widths)]
        w4_w = [keep.tile([P, w], I32, name="w4_w", tag="w4_w%d" % k, align_bytes=64) for k, w in enumerate(widths)]
        wgs_dealt = keep.tile([P, 4, S], F32)
        mix_sb = keep.tile([P, 4, NP], F32)

        nc.vector.memset(tab_s[:].bitcast(I32), 0)
        nc.vector.memset(w4_s[:].bitcast(I32), 0)
        nc.vector.memset(w8_s[:].bitcast(I32), 0)
        nc.vector.memset(vec_rows[:], 0.0)
        make_identity(nc, ident[:])
        make_identity(nc, ident_bf[:])

        def load_scales(dst, row0, src, quadrants):
            for q in quadrants:
                nc.sync.dma_start(
                    out=dst[32 * q + row0 : 32 * q + row0 + 4, :].bitcast(I32).rearrange("r (a c) -> r a c", a=2),
                    in_=src[:, 4 * q : 4 * q + 4, :].bitcast(I32).rearrange("a r c -> r a c"),
                )

        def load_tab_words(a):
            nc.sync.dma_start(out=tab_w[a][:], in_=tab_words[a].rearrange("p t i -> p (t i)").bitcast(I32))

        def load_w1(k, a):
            c0, c1 = CHUNKS[k]
            nc.sync.dma_start(
                out=w1_raw[k][a][:],
                in_=w1[PASS * a : PASS * a + PASS, c0:c1].rearrange("(p i) c -> p i c", i=4),
            )

        def load_packed_weights(k):
            c0, c1 = CHUNKS[k]
            nc.sync.dma_start(
                out=w4_w[k][:].rearrange("p (a c) -> p a c", a=2),
                in_=w4_words.bitcast(I32)[:, :, c0 // 2 : c1 // 2].rearrange("a p c -> p a c"),
            )
            nc.sync.dma_start(
                out=w8_w[k][:].rearrange("p (a c) -> p a c", a=2),
                in_=w8_words.rearrange("a p c i -> a p (c i)").bitcast(I32)[:, :, c0:c1].rearrange("a p c -> p a c"),
            )

        def load_wgs_dealt(t):
            for q in range(4):
                nc.sync.dma_start(
                    out=wgs_dealt[32 * q : 32 * q + 32, t, :], in_=wgs.rearrange("(g t i) j -> t g i j", t=4, i=8)[t]
                )

        def load_page(n):
            if n < PLAIN:
                rows = page0[P * n : P * n + P, :]
            else:
                rows = page0[PASS:H, :].rearrange("(g t i) c -> t g i c", t=4, i=8)[n - PLAIN]
            nc.sync.dma_start(out=page[n][:], in_=rows)

        nc.sync.dma_start(lists[0][:], offs)
        load_tab_words(0)
        load_scales(tab_s, 0, tab_scales, range(0, 4))
        load_scales(w4_s, 0, w4_scales, range(0, 2))
        load_tab_words(1)
        load_scales(w4_s, 0, w4_scales, range(2, 4))
        load_packed_weights(0)
        load_scales(w8_s, 4, w8_scales, range(0, 1))
        load_w1(0, 0)
        load_scales(w8_s, 4, w8_scales, range(1, 3))
        load_w1(0, 1)
        load_scales(w8_s, 4, w8_scales, range(3, 4))
        nc.sync.dma_start(out=wgs_plain[:], in_=wgs)
        load_page(0)
        nc.sync.dma_start(lists[1][:], offs2)
        nc.sync.dma_start(lists[3][:], offs4)
        nc.sync.dma_start(lists[2][:], offs3)
        for row, vec in ((0, gm), (TILES, bl)):
            nc.gpsimd.dma_start(out=vec_rows[row : row + PLAIN, :], in_=vec[0:PASS].rearrange("(n p) -> n p", p=P))
            nc.gpsimd.dma_start(
                out=vec_rows[row + PLAIN : row + TILES, :].rearrange("t (g i) -> t g i", i=8),
                in_=vec[PASS:H].rearrange("(g t i) -> t g i", t=4, i=8),
            )
        for k in (1, 2):
            load_page(k)
            load_w1(k, 0)
            load_w1(k, 1)
            load_packed_weights(k)
        load_page(PLAIN - 1)
        for n in range(PLAIN, TILES):
            load_wgs_dealt(n - PLAIN)
            load_page(n)
        nc.sync.dma_start(out=mix_sb[:], in_=mix.rearrange("(m p) j -> p m j", p=P))

        v_w, v_s = [], []
        for a in range(2):
            v_w.append(keep.tile([P, S], U32, name="v_w%d" % a, align_bytes=64))
            v_s.append(keep.tile([P, S], U8, name="v_s%d" % a, align_bytes=64))

        def gather_words(a, j0, j1):
            entries = lists[0][:, j0 // 16 : j1 // 16]
            nc.vector.tensor_copy(v_w[a][:, j0:j1], tab_w[a][:].bitcast(U32).indirect(entries))

        gather_words(0, 0, S)
        for a in range(2):
            nc.vector.tensor_copy(v_s[a][:], tab_s[:, T * a : T * a + T].indirect(lists[0][:]))

        w1_codes = [keep.tile([P, 2 * P], U32, name="w1_codes%d" % n, align_bytes=64) for n in range(TILES)]
        w1_s = [keep.tile([P, 2 * P], U8, name="w1_s%d" % n, align_bytes=64) for n in range(TILES)]
        w1_bf = {}

        def round_w1(n):
            tag = ("spare0", "spare1", "spare1", "spare0")[n] if n < PLAIN else "slot%d" % (n - PLAIN)
            rounded = keep.tile([P, 2 * PASS], BF16, tag=tag, name="w1_bf", align_bytes=64)
            for a in range(2):
                if n < PLAIN:
                    off = P * (n % 2)
                    src = w1_raw[n // 2][a][:, :, off : off + P].rearrange("p i (g h e) -> p g h i e", h=2, e=4)
                else:
                    src = w1_raw[DEALT][a][:].rearrange("p i (g t h e) -> p t g h i e", t=4, h=2, e=4)[:, n - PLAIN]
                nc.scalar.copy(
                    out=rounded[:, PASS * a : PASS * a + PASS].rearrange("p (g h e i) -> p g h i e", h=2, e=4, i=4),
                    in_=src,
                )
            w1_bf[n] = rounded

        def quantize_w1(n):
            nc.vector.quantize_mx(out=w1_codes[n][:].bitcast(FP8X4), scales=w1_s[n][:], in_=w1_bf[n][:])

        words_dealt = {}
        scales_dealt = {}

        def deal_words():
            for weight, src, run, tag in (("w8", w8_w[DEALT], 8, "spare1"), ("w4", w4_w[DEALT], 4, "spare0")):
                dst = words_dealt[weight] = keep.tile([P, P * run], I32, tag=tag, name="words_dealt", align_bytes=64)
                nc.gpsimd.tensor_copy(
                    out=dst[:].rearrange("p (t g e) -> p t g e", t=4, e=run),
                    in_=src[:].rearrange("p (g t e) -> p t g e", t=4, e=run),
                )

        def deal_scales():
            for weight, src in (("w4", w4_s), ("w8", w8_s)):
                tag = "%s_w%d" % (weight, DEALT)
                dst = scales_dealt[weight] = keep.tile([P, 2 * PASS], U8, tag=tag, name="scales_dealt", align_bytes=64)
                nc.gpsimd.tensor_copy(
                    out=dst[:].bitcast(I32).rearrange("p (t a g e) -> p t a g e", t=4, a=2, e=2),
                    in_=src[:].bitcast(I32).rearrange("p (a b g t e) -> p b t a g e", a=2, b=2, t=4, e=2)[:, 1],
                )

        def weight_operands(weight, n, a):
            if weight == "w1":
                return w1_codes[n][:, P * a : P * a + P].bitcast(FP8X4), w1_s[n][:, P * a : P * a + P]
            if n < PLAIN:
                col0 = 2 * P * a + P * (n % 2)
                word_cols = slice(col0, col0 + P)
                scale_cols = slice(H * a + P * n, H * a + P * n + P)
                words4, words8, scales4, scales8 = w4_w[n // 2], w8_w[n // 2], w4_s, w8_s
            else:
                col0 = 2 * P * (n - PLAIN) + P * a
                word_cols = scale_cols = slice(col0, col0 + P)
                words4, words8 = words_dealt["w4"], words_dealt["w8"]
                scales4, scales8 = scales_dealt["w4"], scales_dealt["w8"]
            if weight == "w4":
                return words4[:].bitcast(U8)[:, 2 * col0 : 2 * col0 + 2 * P].bitcast(FP4X4), scales4[:, scale_cols]
            return words8[:, word_cols].bitcast(FP8X4), scales8[4:P, scale_cols]

        product, w4_product_sb, two_max, h = {}, {}, {}, {}

        def multiply(n, weights):
            for weight in weights:
                product[n, weight] = psum.tile([P, S], F32, tag=weight, name="product", bufs=1)
            for a in range(2):
                for weight in weights:
                    words, scales = weight_operands(weight, n, a)
                    nc.tensor.matmul_mx(
                        out=product[n, weight][:], lhsT=words, lhsT_scale=scales,
                        rhs=v_w[a][:].bitcast(FP8X4), rhs_scale=v_s[a][:], start=(a == 0), stop=(a == 1),
                    )

        def copy_w4_product(n):
            w4_product_sb[n] = ring.tile([P, S], F32, tag="turn%d" % (n % 2), name="w4_product_sb", bufs=1)
            nc.scalar.copy(out=w4_product_sb[n][:], in_=product[n, "w4"][:])

        def max_of_two(n):
            tag = "spare0" if n == 1 else "slot%d" % (n - 2)
            two_max[n] = keep.tile([P, S], F32, tag=tag, name="two_max", align_bytes=64)
            nc.vector.tensor_tensor(two_max[n][:], product[n, "w8"][:], w4_product_sb[n][:], ALU.max)

        def max_of_three(n):
            h[n] = ring.tile([P, S], F32, tag="h", name="h", bufs=1, align_bytes=64)
            nc.vector.tensor_tensor(h[n][:], product[n, "w1"][:], two_max[n][:], ALU.max)

        def scatter(n):
            factor = wgs_plain[:] if n < PLAIN else wgs_dealt[:, n - PLAIN, :]
            nc.vector.tensor_tensor(page[n][:].indirect(lists[1][:]), h[n][:], factor, ALU.mult)

        vec_cols = keep.tile([P, 2 * TILES], F32)

        def turn_vectors():
            turned_vecs = psum.tile([P, P], F32, tag="w1", name="turned_vecs", bufs=1)
            nc.tensor.transpose(turned_vecs[:], vec_rows[:], ident[:])
            nc.scalar.copy(out=vec_cols[:], in_=turned_vecs[:, 0 : 2 * TILES])

        x_pairs = [keep.tile([P, 4, 2, P], F32, name="x_pairs%d" % v) for v in range(2)]
        x_dealt = [keep.tile([P, 4 * NP], BF16, name="x_dealt%d" % v, align_bytes=64) for v in range(2)]

        def fetch(n, v, c0, c1, fetched):
            got = fetched[:, NP * v + P * c0 : NP * v + P * c1]
            nc.vector.tensor_copy(got, page[n][:].indirect(lists[2 + v][:, 8 * c0 : 8 * c1]))
            if n < PLAIN:
                x_bf = ring.tile([P, NP], BF16, tag="x_bf", name="x_bf", bufs=3)
                dst = x_bf[:]
            else:
                dst = x_dealt[v][:].rearrange("p (c t) -> p c t", t=4)[:, P * c0 : P * c1, n - PLAIN]
            if v == X1:
                nc.scalar.activation(dst, got, ACT.Copy, scale=vec_cols[:, n : n + 1])
            else:
                nc.scalar.activation(dst, got, ACT.Identity, bias=vec_cols[:, TILES + n : TILES + n + 1])
            if n < PLAIN:
                turned = psum.tile([P, 4, P], BF16, tag="turned", name="turned")
                for c in range(4):
                    nc.tensor.transpose(turned[:, c, :], x_bf[:, P * c : P * c + P], ident_bf[:])
                nc.scalar.copy(
                    out=x_pairs[v][:, :, :, 32 * n : 32 * n + 32],
                    in_=turned[:].bitcast(F32).rearrange("m c (p u) -> m c u p", u=2),
                )

        def turn_back(v):
            pairs = keep.tile([P, 2 * NP], F32, name="x_turned_back%d" % v, align_bytes=64)
            for c in (0, 2):
                back = psum.tile([P, 2, 2, P], F32, tag="back", name="back")
                for d in range(2):
                    for u in range(2):
                        nc.tensor.transpose(back[:, d, u, :], x_pairs[v][:, c + d, u, :], ident[:])
                nc.scalar.copy(
                    out=pairs[:, 2 * P * c : 2 * P * (c + 2)].rearrange("p (d m u) -> p d m u", d=2, u=2),
                    in_=back[:].rearrange("p d u m -> p d m u"),
                )
            return pairs

        x_s = [[keep.tile([P, NP], U8, name="x_s%d%d" % (b, v), align_bytes=64) for v in range(2)] for b in range(2)]
        x_codes = [
            [keep.tile([P, NP], U32, name="x_codes%d%d" % (b, v), align_bytes=64) for v in range(2)] for b in range(2)
        ]

        def quantize_x(b, v, c0, c1, values):
            cols = slice(P * c0, P * c1)
            nc.vector.quantize_mx(out=x_codes[b][v][:, cols].bitcast(FP8X4), scales=x_s[b][v][:, cols], in_=values)

        round_w1(0)
        quantize_w1(0)
        halves = (slice(0, S // 2), slice(S // 2, S))
        first = {}
        for half, tags in zip(halves, ((("w4", 1), ("w8", 1), ("w1", 1)), (("back", 2), ("back", 2), ("extra", 1)))):
            gather_words(1, half.start, half.stop)
            for weight, (tag, bufs) in zip(WEIGHTS, tags):
                first[half.start, weight] = psum.tile([P, S // 2], F32, tag=tag, name="first", bufs=bufs)
            for a in range(2):
                for weight in WEIGHTS:
                    words, scales = weight_operands(weight, 0, a)
                    nc.tensor.matmul_mx(
                        out=first[half.start, weight][:], lhsT=words, lhsT_scale=scales,
                        rhs=v_w[a][:, half].bitcast(FP8X4), rhs_scale=v_s[a][:, half], start=(a == 0), stop=(a == 1),
                    )
        round_w1(1)
        first_sb = keep.tile([P, S], F32, tag="w1_raw01", name="first_sb")
        first_two = keep.tile([P, S], F32, tag="spare0", name="first_two", align_bytes=64)
        h[0] = ring.tile([P, S], F32, tag="h", name="h", bufs=1, align_bytes=64)
        for half in halves:
            nc.scalar.copy(out=first_sb[:, half], in_=first[half.start, "w4"][:])
        for half in halves:
            nc.vector.tensor_tensor(first_two[:, half], first[half.start, "w8"][:], first_sb[:, half], ALU.max)
        for half in halves:
            nc.vector.tensor_tensor(h[0][:, half], first[half.start, "w1"][:], first_two[:, half], ALU.max)
        for half in halves:
            places = lists[1][:, half.start // 16 : half.stop // 16]
            nc.vector.tensor_tensor(page[0][:].indirect(places), h[0][:, half], wgs_plain[:, half], ALU.mult)
        quantize_w1(1)
        turn_vectors()
        multiply(1, WEIGHTS)
        copy_w4_product(1)
        round_w1(2)

        turned_back = {}
        for n in range(TILES):
            if n > 0:
                scatter(n)
            if n + 1 < TILES:
                max_of_two(n + 1)
            if n + 2 < TILES:
                quantize_w1(n + 2)
                multiply(n + 2, ("w4",))
            fetched = ring.tile([P, 2 * NP], F32, tag="turn%d" % ((n + 1) % 2), name="fetched", bufs=1)
            if n < LAST:
                fetch(n, X2, 0, 4, fetched)
            if n + 2 < TILES:
                multiply(n + 2, ("w8",))
            if n + 1 < TILES:
                max_of_three(n + 1)
            if n + 2 < TILES:
                multiply(n + 2, ("w1",))
            if n + 3 < TILES:
                round_w1(n + 3)
            if n < LAST:
                fetch(n, X1, 0, 4, fetched)
            if n + 2 < TILES:
                copy_w4_product(n + 2)
            if n == PLAIN:
                turned_back[X2] = turn_back(X2)
            if n == PLAIN + 1:
                turned_back[X1] = turn_back(X1)
            if n == PLAIN - 3:
                deal_words()
                deal_scales()
            if n == PLAIN + 1:
                quantize_x(0, X2, 0, 4, turned_back[X2][:].bitcast(BF16))
            if n == PLAIN + 2:
                quantize_x(0, X1, 0, 4, turned_back[X1][:].bitcast(BF16))

        for v, c0, c1 in LAST_PIECES:
            fetch(LAST, v, c0, c1, fetched)

        banks = (("w4", 1), ("w8", 1), ("w1", 1), ("extra", 1), ("back", 2), ("back", 2), ("turned", 2), ("turned", 2))
        e = [psum.tile([P, PART], F32, tag=tag, name="e", bufs=bufs) for tag, bufs in banks]
        parts = range(len(OUT_PARTS))

        def score(b, part):
            m, j0 = OUT_PARTS[part]
            peaks, compounds = slice(P * m, P * m + P), slice(j0, j0 + PART)
            nc.tensor.matmul_mx(
                out=e[part][:], lhsT=x_codes[b][X1][:, peaks].bitcast(FP8X4), lhsT_scale=x_s[b][X1][:, peaks],
                rhs=x_codes[b][X2][:, compounds].bitcast(FP8X4), rhs_scale=x_s[b][X2][:, compounds],
                start=(b == 0), stop=(b == 1),
            )

        for part in parts:
            score(0, part)
        for v, c0, c1 in LAST_PIECES:
            quantize_x(1, v, c0, c1, x_dealt[v][:, 4 * P * c0 : 4 * P * c1])
        tanh_e = []
        for part in parts:
            score(1, part)
            tanh_e.append(keep.tile([P, PART], F32, name="tanh_e%d" % part))
            nc.scalar.activation(tanh_e[part][:], e[part][:], ACT.Tanh)
        weighed = []

        def weigh(part):
            m, j0 = OUT_PARTS[part]
            weighed.append(ring.tile([P, PART], F32, tag="weighed", name="weighed"))
            nc.vector.tensor_tensor(weighed[part][:], tanh_e[part][:], mix_sb[:, m, j0 : j0 + PART], ALU.mult)

        def finish(part):
            m, j0 = OUT_PARTS[part]
            result = keep.tile([P, PART], F32, name="result%d" % part)
            nc.vector.tensor_tensor(result[:], e[part][:], weighed[part][:], ALU.add)
            nc.sync.dma_start(out=out[P * m : P * m + P, j0 : j0 + PART], in_=result[:])

        weigh(0)
        for part in parts:
            if part + 1 < len(parts):
                weigh(part + 1)
            finish(part)
